import numpy as np
import ml_dtypes


def mxq(x, axis, fmt="e4m3"):
    dtype, down = {"e4m3": (ml_dtypes.float8_e4m3fn, 7), "e5m2": (ml_dtypes.float8_e5m2, 14)}[fmt]
    v = np.moveaxis(np.asarray(x, np.float32).astype(ml_dtypes.bfloat16).astype(np.float64), axis, -1)
    blocks = v.reshape(v.shape[:-1] + (-1, 32))
    amax = np.abs(blocks).max(-1, keepdims=True)
    byte = np.maximum(np.where(amax > 0, np.frexp(amax)[1] - 1 + 127, 0) - down, 1)
    scale = np.exp2(byte - 127.0)
    codes = (blocks / scale).astype(np.float32).astype(dtype).astype(np.float64)
    return np.moveaxis((codes * scale).reshape(v.shape), -1, axis)


WIDE = False


def mx_kscale(k):
    if not WIDE:
        return np.ones(k)
    levels = np.array([10, -10, 5, -5, 0])
    if k % 512:
        return np.exp2(np.random.permutation(np.resize(levels, k // 32))).repeat(32)
    a = np.empty((k // 512, 16))
    for p in range(k // 512):
        a[p, :8] = np.random.permutation(np.resize(levels, 8))
        for g in range(8):
            far = levels[np.abs(levels - a[p, g]) >= 10]
            a[p, g + 8] = far[np.random.randint(len(far))]
    return np.exp2(a.ravel()).repeat(32)


def f64(x):
    return np.asarray(x).astype(np.float64)


def striped(idx):
    return np.tile(idx.reshape(-1, 16).T, (8, 1)).astype(np.uint16)


def unstriped(offs):
    return offs[:16].T.reshape(-1).astype(np.int64)


E2M1 = np.array([0.0, 0.5, 1.0, 1.5, 2.0, 3.0, 4.0, 6.0, -0.0, -0.5, -1.0, -1.5, -2.0, -3.0, -4.0, -6.0])


def pack_weight(w, fmt):
    k, n = w.shape
    w = f64(np.asarray(w, np.float32).astype(ml_dtypes.bfloat16)).reshape(k // 32, 32, n)
    amax = np.abs(w).max(1)
    if fmt == "e4m3":
        byte = np.frexp(amax)[1] - 1 + 127 - 7
    else:
        mant, ex = np.frexp(amax / 6.0)
        byte = np.where(mant > 0.5, ex, ex - 1) + 127
    byte = np.clip(np.where(amax > 0, byte, 1), 1, 254)
    scaled = (w * np.exp2(127.0 - byte)[:, None, :]).reshape(k, n).astype(np.float32)
    by_word = np.ascontiguousarray(scaled.reshape(k // 512, 128, 4, n).transpose(0, 1, 3, 2))
    if fmt == "e4m3":
        words = by_word.astype(ml_dtypes.float8_e4m3fn).view(np.uint8)
    else:
        c = by_word.astype(ml_dtypes.float4_e2m1fn).view(np.uint8) & 0xF
        words = (c[..., 0::2] | (c[..., 1::2] << 4)).reshape(k // 512, 128, 2 * n)
    return np.ascontiguousarray(words), np.ascontiguousarray(byte.astype(np.uint8).reshape(k // 512, 16, n))


def unpack_weight(words, scales, fmt):
    g, _, n = scales.shape
    words = np.ascontiguousarray(words).reshape(g, 128, n, -1)
    if fmt == "e4m3":
        vals = words.view(ml_dtypes.float8_e4m3fn).astype(np.float64)
    else:
        nib = np.empty((g, 128, n, 4), np.uint8)
        nib[..., 0::2] = words & 0xF
        nib[..., 1::2] = words >> 4
        vals = E2M1[nib]
    vals = vals * np.repeat(np.exp2(scales.astype(np.float64) - 127.0), 8, axis=1)[..., None]
    return vals.transpose(0, 1, 3, 2).reshape(g * 512, n)


def gelu(v):
    return 0.5 * v * (1.0 + np.tanh(np.sqrt(2.0 / np.pi) * (v + 0.044715 * v**3)))


K, T, S, H, T2, P = 1024, 2048, 512, 1024, 1024, 512

def setup_inputs():
    n = np.random.standard_normal
    s = mx_kscale(K)[:, None]
    u = mx_kscale(H)[:, None]
    d = {}
    d["tab_words"], d["tab_scales"] = pack_weight(n((K, T)) * s, "e4m3")
    d["offs"] = striped(np.random.permutation(T)[:S])
    d["w1"] = (0.7 * n((K, H)) / K ** 0.5 / s).astype(np.float32)
    d["w4_words"], d["w4_scales"] = pack_weight(0.58 * n((K, H)) / K ** 0.5 / s, "e2m1")
    d["amp"] = (2.0 * n((H, S))).astype(np.float32)
    d["gain"] = (np.exp(0.3 * n(H)) * u[:, 0]).astype(np.float32)
    d["page0"] = (n((H, T2)) * u).astype(np.float32)
    d["wgs"] = np.exp(0.3 * n((128, S))).astype(np.float32)
    d["offs2"] = striped(np.random.permutation(T2)[:S])
    d["offs3"] = striped(np.random.permutation(T2)[:P])
    d["base"] = (0.8 * n((H, P)) * u).astype(np.float32)
    d["qv"] = (np.exp(0.4 * n(H)) / H ** 0.5 / u[:, 0] ** 2).astype(np.float32)
    d["slot"] = (0.8 * n(T2)).astype(np.float32)
    return d

def reference(tab_words, tab_scales, offs, w1, w4_words, w4_scales, amp, gain, page0, wgs, offs2, offs3, base, qv, slot):
    v = unpack_weight(tab_words, tab_scales, "e4m3")[:, unstriped(offs)]
    a = mxq(f64(w1), 0, "e4m3").T @ v
    b = unpack_weight(w4_words, w4_scales, "e2m1").T @ v
    h = (np.sin(b) * f64(amp) + a) * f64(gain)[:, None]
    page = f64(page0).copy()
    page[:, unstriped(offs2)] = np.tile(f64(wgs), (H // 128, 1)) * h
    x = page[:, unstriped(offs3)]
    x = (np.abs(x) + f64(base)) * f64(qv)[:, None]
    e = mxq(page, 0, "e4m3").T @ mxq(x, 0, "e4m3")
    return np.maximum(e, f64(slot)[:, None])

@@ -1,0 +1,329 @@
+import math
+from contextlib import ExitStack
+
+import concourse.mybir as mybir
+
+K, T, S, H, T2, PX = 1024, 2048, 512, 1024, 1024, 512
+FLOPS = 2 * K * H * S * 2 + 2 * H * T2 * PX
+
+F32 = mybir.dt.float32
+BF16 = mybir.dt.bfloat16
+I32 = mybir.dt.int32
+U32 = mybir.dt.uint32
+U16 = mybir.dt.uint16
+U8 = mybir.dt.uint8
+FP8X4 = mybir.dt.float8_e4m3fn_x4
+FP4X4 = mybir.dt.float4_e2m1fn_x4
+ALU = mybir.AluOpType
+ACT = mybir.ActivationFunctionType
+
+P = 128
+ROUNDER = 12582912.0
+TWO_PI = 2.0 * math.pi
+USE_POOL = False
+
+
+def tile_list_blade_noise_page_kernel(tc, tab_words, tab_scales, offs, w1, w4_words, w4_scales, amp, gain,
+                                                page0, wgs, offs2, offs3, base, qv, slot, out):
+    nc = tc.nc
+    with ExitStack() as ctx:
+        keep = ctx.enter_context(tc.tile_pool(name="keep", bufs=1))
+        big = ctx.enter_context(tc.tile_pool(name="big", bufs=6))
+        mid = ctx.enter_context(tc.tile_pool(name="mid", bufs=4))
+        ring = ctx.enter_context(tc.tile_pool(name="ring", bufs=2))
+        psum = ctx.enter_context(tc.psum_pool(name="psum", bufs=1))
+
+        warm = keep.tile([P, 1], F32, name="warm")
+        nc.vector.memset(warm[:], 0.0)
+        nc.scalar.activation(warm[:], warm[:], ACT.Sin)
+
+        tab_s = keep.tile([P, 2, T], U8, name="tab_s", align_bytes=64)
+        w4_s = keep.tile([P, 2, H], U8, name="w4_s", align_bytes=64)
+        nc.vector.memset(tab_s[:].rearrange("p a n -> p (a n)").bitcast(I32), 0)
+        nc.gpsimd.memset(w4_s[:].rearrange("p a n -> p (a n)").bitcast(I32), 0)
+
+        list1 = keep.tile([P, S // 16], U16, name="list1")
+        list2 = keep.tile([P, S // 16], U16, name="list2")
+        list3 = keep.tile([P, PX // 16], U16, name="list3")
+        gain_c = keep.tile([P, 2, 4], F32, name="gain_c")
+        qv_c = keep.tile([P, 2, 4], F32, name="qv_c")
+        slot_c = keep.tile([P, 8], F32, name="slot_c")
+        wgs_first = keep.tile([P, S], F32, name="wgs_first")
+        wgs_rest = keep.tile([P, 3, S], F32, name="wgs_rest")
+        wgs_rows = wgs.rearrange("(p t) j -> p t j", t=4)
+        tab_w = [big.tile([P, T], I32, name="tab_w", tag="big", align_bytes=64) for a in range(2)]
+        w4_w = [keep.tile([P, 2, H], U8, name="w4_w%d" % b, align_bytes=64) for b in range(2)]
+
+        def load_w4(b):
+            nc.sync.dma_start(w4_w[b][:].bitcast(I32), w4_words[:, :, H * b : H * (b + 1)].rearrange("a p n -> p a n").bitcast(I32))
+
+        def load_tab(a):
+            nc.sync.dma_start(tab_w[a][:], tab_words[a].rearrange("p n i -> p (n i)").bitcast(I32))
+
+        nc.sync.dma_start(list1[:], offs)
+        nc.sync.dma_start(list2[:], offs2)
+        nc.sync.dma_start(list3[:], offs3)
+        nc.sync.dma_start(gain_c[:], gain.rearrange("(b p t) -> p b t", b=2, t=4))
+        nc.sync.dma_start(qv_c[:], qv.rearrange("(b p t) -> p b t", b=2, t=4))
+        load_w4(0)
+        load_tab(0)
+        for q in range(1):
+            nc.sync.dma_start(wgs_first[32 * q : 32 * (q + 1), :], wgs_rows[:, 0, :])
+        for q in range(4):
+            nc.sync.dma_start(tab_s[32 * q : 32 * q + 4, :, :].bitcast(I32),
+                              tab_scales[:, 4 * q : 4 * q + 4, :].rearrange("a r n -> r a n").bitcast(I32))
+        load_tab(1)
+        for q in range(4):
+            nc.sync.dma_start(w4_s[32 * q : 32 * q + 4, :, :].bitcast(I32),
+                              w4_scales[:, 4 * q : 4 * q + 4, :].rearrange("a r n -> r a n").bitcast(I32))
+
+        w1_raw = {}
+
+        def load_w1(b):
+            for a in range(2):
+                raw = big.tile([P, 4, 512], F32, name="w1_raw", tag="big", align_bytes=64)
+                nc.sync.dma_start(raw[:], w1[512 * a : 512 * (a + 1), 512 * b : 512 * (b + 1)].rearrange("(p j) c -> p j c", j=4))
+                w1_raw[b, a] = raw
+
+        load_w1(0)
+        load_w4(1)
+        amp_rows = amp.rearrange("(b p t) j -> b t p j", b=2, t=4)
+        page_rows = page0.rearrange("(b p t) m -> b t p m", b=2, t=4)
+        amp_t = [keep.tile([P, S], F32, name="amp%d" % n) for n in range(8)]
+        page = [keep.tile([P, T2], F32, name="page%d" % n) for n in range(8)]
+        base_t = [keep.tile([P, 4, PX], F32, name="base%d" % b) for b in range(2)]
+
+        def load_tile(n):
+            nc.sync.dma_start(amp_t[n][:], amp_rows[n // 4, n % 4])
+            if n == 0:
+                for q in range(1, 4):
+                    nc.sync.dma_start(wgs_first[32 * q : 32 * (q + 1), :], wgs_rows[:, 0, :])
+            if n == 1:
+                for q in range(4):
+                    nc.sync.dma_start(wgs_rest[32 * q : 32 * (q + 1), :, :], wgs_rows[:, 1:4, :])
+            nc.sync.dma_start(page[n][:], page_rows[n // 4, n % 4])
+            if n == 1:
+                nc.sync.dma_start(base_t[0][:], base[0:512, :].rearrange("(p t) j -> p t j", t=4))
+            if n == 2:
+                load_w1(1)
+            if n == 4:
+                nc.sync.dma_start(base_t[1][:], base[512:1024, :].rearrange("(p t) j -> p t j", t=4))
+
+        for n in range(8):
+            load_tile(n)
+        with nc.allow_non_contiguous_dma(reason="one value a partition"):
+            nc.sync.dma_start(slot_c[:], slot.rearrange("(c p) -> p c", p=P))
+
+        v_w = keep.tile([P, 2, S], U32, name="v_w", align_bytes=64)
+        v_s = keep.tile([P, 2, S], U8, name="v_s", align_bytes=64)
+        nc.vector.tensor_copy(v_w[:, 0, :], tab_w[0][:].bitcast(U32).indirect(list1[:]))
+        for a in range(2):
+            nc.vector.tensor_copy(v_s[:, a, :], tab_s[:, a, :].indirect(list1[:]))
+        nc.vector.tensor_copy(v_w[:, 1, :], tab_w[1][:].bitcast(U32).indirect(list1[:]))
+
+        w4_wd = [keep.tile([P, 2, 4, 256], U8, name="w4_wd%d" % b, align_bytes=64) for b in range(2)]
+        w4_sd = [keep.tile([P, 2, 4, P], U8, name="w4_sd%d" % b, align_bytes=64) for b in range(2)]
+
+        def deal_w4(b):
+            nc.vector.tensor_copy(w4_wd[b][:].bitcast(U16), w4_w[b][:].bitcast(U16).rearrange("p a (q t) -> p a t q", t=4))
+            nc.vector.tensor_copy(w4_sd[b][:], w4_s[:, :, 512 * b : 512 * (b + 1)].rearrange("p a (q t) -> p a t q", t=4))
+
+        w1_c = keep.tile([P, 2, 2, 512], U32, name="w1_c", align_bytes=64)
+        w1_s = keep.tile([P, 2, 2, 512], U8, name="w1_s", align_bytes=64)
+        w1_g = {}
+
+        def weave_w1(b, a, on_vector):
+            g = mid.tile([P, 4, P, 4], BF16, name="w1_g", tag="mid", align_bytes=64)
+            dst = g[:].rearrange("p t q j -> p q j t")
+            src = w1_raw[b, a][:].rearrange("p j (q t) -> p q j t", t=4)
+            if on_vector:
+                nc.vector.tensor_copy(dst, src)
+            else:
+                for half in range(2):
+                    nc.scalar.copy(dst[:, 64 * half : 64 * (half + 1)], src[:, 64 * half : 64 * (half + 1)])
+            w1_g[b, a] = g
+
+        def quant_w1(b, a):
+            nc.vector.quantize_mx(out=w1_c[:, b, a, :].bitcast(FP8X4), scales=w1_s[:, b, a, :],
+                                  in_=w1_g[b, a][:].rearrange("p t q j -> p (t q j)"))
+
+        work = [keep.tile([P, S], F32, name="work%d" % n) for n in range(8)]
+
+        def phase(n):
+            b, t = divmod(n, 4)
+            acc = psum.tile([P, S], F32, name="acc_b", tag="acc_b", bufs=3)
+            for a in range(2):
+                nc.tensor.matmul_mx(acc[:], lhsT=w4_wd[b][:, a, t, :].bitcast(FP4X4), lhsT_scale=w4_sd[b][:, a, t, :],
+                                    rhs=v_w[:, a, :].bitcast(FP8X4), rhs_scale=v_s[:, a, :], start=(a == 0), stop=(a == 1))
+            turns = ring.tile([P, S], U32, name="turns")
+            nc.scalar.activation(turns[:], acc[:], ACT.Copy, bias=ROUNDER, scale=1.0 / TWO_PI)
+            whole = ring.tile([P, S], F32, name="whole")
+            nc.scalar.activation(whole[:], turns[:], ACT.Copy, bias=-ROUNDER, scale=1.0)
+            nc.vector.scalar_tensor_tensor(work[n][:], whole[:], -TWO_PI, acc[:], ALU.mult, ALU.add)
+
+        def sine(n):
+            nc.scalar.activation(work[n][:], work[n][:], ACT.Sin)
+
+        def pre_amp(n):
+            b, t = divmod(n, 4)
+            nc.gpsimd.tensor_scalar(amp_t[n][:], amp_t[n][:], gain_c[:, b, t : t + 1], 0.0, ALU.mult, ALU.add)
+
+        def times_amp(n):
+            b, t = divmod(n, 4)
+            if USE_POOL:
+                nc.gpsimd.tensor_tensor(work[n][:], work[n][:], amp_t[n][:], ALU.mult)
+            else:
+                nc.vector.scalar_tensor_tensor(work[n][:], work[n][:], gain_c[:, b, t : t + 1], amp_t[n][:], ALU.mult, ALU.mult)
+
+        def direct(n):
+            b, t = divmod(n, 4)
+            acc = psum.tile([P, S], F32, name="acc_a", tag="acc_a", bufs=2)
+            cols = slice(P * t, P * (t + 1))
+            for a in range(2):
+                nc.tensor.matmul_mx(acc[:], lhsT=w1_c[:, b, a, cols].bitcast(FP8X4), lhsT_scale=w1_s[:, b, a, cols],
+                                    rhs=v_w[:, a, :].bitcast(FP8X4), rhs_scale=v_s[:, a, :], start=(a == 0), stop=(a == 1))
+            nc.vector.scalar_tensor_tensor(work[n][:], acc[:], gain_c[:, b, t : t + 1], work[n][:], ALU.mult, ALU.add)
+
+        def wgs_of(t):
+            return wgs_first[:] if t == 0 else wgs_rest[:, t - 1, :]
+
+        def times_wgs(n):
+            nc.gpsimd.tensor_tensor(work[n][:], work[n][:], wgs_of(n % 4), ALU.mult)
+
+        picked = {}
+
+        def put_and_pick(n):
+            if USE_POOL:
+                nc.vector.tensor_copy(page[n][:].indirect(list2[:]), work[n][:])
+            else:
+                nc.vector.tensor_tensor(page[n][:].indirect(list2[:]), work[n][:], wgs_of(n % 4), ALU.mult)
+            g = work[n]
+            nc.vector.tensor_copy(g[:], page[n][:].indirect(list3[:]))
+            picked[n] = g
+
+        page_pairs = {}
+        x_pairs = {}
+
+        def round_page(n):
+            b, t = divmod(n, 4)
+            if t == 0:
+                page_pairs[b] = big.tile([P, 2, T2, 2], BF16, name="page_pairs", tag="big", align_bytes=64)
+            nc.scalar.copy(page_pairs[b][:, t // 2, :, t % 2], page[n][:])
+
+        def magnitude(n):
+            nc.scalar.activation(picked[n][:], picked[n][:], ACT.Abs)
+
+        def plus_base(n):
+            b, t = divmod(n, 4)
+            eng = nc.gpsimd if USE_POOL else nc.vector
+            eng.tensor_tensor(picked[n][:], picked[n][:], base_t[b][:, t, :], ALU.add)
+
+        def round_x(n):
+            b, t = divmod(n, 4)
+            if t == 0:
+                x_pairs[b] = mid.tile([P, 2, PX, 2], BF16, name="x_pairs", tag="mid", align_bytes=64)
+            nc.scalar.activation(x_pairs[b][:, t // 2, :, t % 2], picked[n][:], ACT.Copy, scale=qv_c[:, b, t : t + 1])
+
+        page_c = keep.tile([P, 2, T2], U32, name="page_c", align_bytes=64)
+        page_s = keep.tile([P, 2, T2], U8, name="page_s", align_bytes=64)
+        x_c = keep.tile([P, 2, PX], U32, name="x_c", align_bytes=64)
+        x_s = keep.tile([P, 2, PX], U8, name="x_s", align_bytes=64)
+
+        def weave(dst, src, on_vector):
+            d = dst[:].bitcast(F32)
+            s = src[:].rearrange("p u c e -> p u (c e)").bitcast(F32).rearrange("p u c -> p c u")
+            if on_vector:
+                nc.vector.tensor_copy(d, s)
+            else:
+                nc.scalar.copy(d, s)
+
+        woven = {}
+
+        def weave_page(b, on_vector):
+            g = big.tile([P, T2, 4], BF16, name="page_g", tag="big", align_bytes=64)
+            weave(g, page_pairs[b], on_vector)
+            woven["p", b] = g
+
+        def weave_x(b, on_vector):
+            g = mid.tile([P, PX, 4], BF16, name="x_g", tag="mid", align_bytes=64)
+            weave(g, x_pairs[b], on_vector)
+            woven["x", b] = g
+
+        def quant_page(b):
+            nc.vector.quantize_mx(out=page_c[:, b, :].bitcast(FP8X4), scales=page_s[:, b, :],
+                                  in_=woven["p", b][:].rearrange("p c t -> p (c t)"))
+
+        def quant_x(b):
+            nc.vector.quantize_mx(out=x_c[:, b, :].bitcast(FP8X4), scales=x_s[:, b, :],
+                                  in_=woven["x", b][:].rearrange("p c t -> p (c t)"))
+
+        def scale_base(t):
+            nc.scalar.activation(base_t[1][:, t, :], base_t[1][:, t, :], ACT.Copy, scale=qv_c[:, 1, t : t + 1])
+
+        def finish_x(n):
+            b, t = divmod(n, 4)
+            nc.vector.scalar_tensor_tensor(x_pairs[b][:, t // 2, :, t % 2], work[n][:], qv_c[:, b, t : t + 1], base_t[b][:, t, :], ALU.mult, ALU.add)
+
+        def last_tile():
+            b, t, n = 1, 3, 7
+            g = big.tile([P, T2, 4], BF16, name="page_g", tag="big", align_bytes=64)
+            words = page_pairs[b][:].rearrange("p u c e -> p u (c e)").bitcast(F32).rearrange("p u c -> p c u")
+            nc.vector.scalar_tensor_tensor(work[n][:], work[n][:], -1.0, work[n][:], ALU.mult, ALU.max)
+            finish_x(n)
+            weave_x(b, True)
+            for half in range(2):
+                cols = slice(512 * half, 512 * (half + 1))
+                nc.scalar.copy(page_pairs[b][:, 1, cols, 1], page[n][:, cols])
+                nc.scalar.copy(g[:].bitcast(F32)[:, cols, :], words[:, cols, :])
+                if half == 1:
+                    quant_x(b)
+                nc.vector.quantize_mx(out=page_c[:, b, cols].bitcast(FP8X4), scales=page_s[:, b, cols],
+                                      in_=g[:, cols, :].rearrange("p c t -> p (c t)"))
+
+        deal_w4(0)
+        phase(0)
+        phase(1)
+        sine(0)
+        weave_w1(0, 0, False)
+        weave_w1(0, 1, True)
+        quant_w1(0, 0)
+        quant_w1(0, 1)
+        deal_w4(1)
+        for n in range(8):
+            times_amp(n)
+            direct(n)
+            put_and_pick(n)
+            if n + 1 < 8:
+                sine(n + 1)
+            if n + 2 < 8:
+                phase(n + 2)
+            if n in (1, 2):
+                weave_w1(1, n - 1, False)
+                quant_w1(1, n - 1)
+            if n in (4, 5):
+                scale_base(n - 2)
+            if n < 7:
+                round_page(n)
+                magnitude(n)
+            if n < 6:
+                plus_base(n)
+                round_x(n)
+            if n == 6:
+                finish_x(n)
+            if n == 3:
+                weave_page(0, False)
+                weave_x(0, False)
+                quant_page(0)
+                quant_x(0)
+        last_tile()
+
+        for c in range(8):
+            tag, bufs = (("acc_o", 3), ("acc_b", 3), ("acc_a", 2))[c // 3]
+            acc = psum.tile([P, PX], F32, name="acc_o", tag=tag, bufs=bufs)
+            cols = slice(P * c, P * (c + 1))
+            for b in range(2):
+                nc.tensor.matmul_mx(acc[:], lhsT=page_c[:, b, cols].bitcast(FP8X4), lhsT_scale=page_s[:, b, cols],
+                                    rhs=x_c[:, b, :].bitcast(FP8X4), rhs_scale=x_s[:, b, :], start=(b == 0), stop=(b == 1))
+            res = amp_t[c]
+            nc.vector.tensor_scalar(res[:], acc[:], slot_c[:, c : c + 1], None, ALU.max)
+            nc.sync.dma_start(out[cols, :], res[:])

@@ -20,7 +20,13 @@ ACT = mybir.ActivationFunctionType
 P = 128
 ROUNDER = 12582912.0
 TWO_PI = 2.0 * math.pi
-USE_POOL = False
+USE_POOL = True
+NB = 4
+AHEAD = 4
+LAG = 2
+YLAG = 2
+HOLD_P = 6
+HOLD_X = 7
 
 
 def tile_list_blade_noise_page_kernel(tc, tab_words, tab_scales, offs, w1, w4_words, w4_scales, amp, gain,
@@ -30,7 +36,7 @@ def tile_list_blade_noise_page_kernel(tc, tab_words, tab_scales, offs, w1, w4_wo
         keep = ctx.enter_context(tc.tile_pool(name="keep", bufs=1))
         big = ctx.enter_context(tc.tile_pool(name="big", bufs=6))
         mid = ctx.enter_context(tc.tile_pool(name="mid", bufs=4))
-        ring = ctx.enter_context(tc.tile_pool(name="ring", bufs=2))
+        ring = ctx.enter_context(tc.tile_pool(name="ring", bufs=3))
         psum = ctx.enter_context(tc.psum_pool(name="psum", bufs=1))
 
         warm = keep.tile([P, 1], F32, name="warm")
@@ -57,6 +63,13 @@ def tile_list_blade_noise_page_kernel(tc, tab_words, tab_scales, offs, w1, w4_wo
         def load_w4(b):
             nc.sync.dma_start(w4_w[b][:].bitcast(I32), w4_words[:, :, H * b : H * (b + 1)].rearrange("a p n -> p a n").bitcast(I32))
 
+        w1_raw = {}
+
+        def load_w1_pass(b, a):
+            raw = big.tile([P, 4, 512], F32, name="w1_raw", tag="big", align_bytes=64)
+            nc.sync.dma_start(raw[:], w1[512 * a : 512 * (a + 1), 512 * b : 512 * (b + 1)].rearrange("(p j) c -> p j c", j=4))
+            w1_raw[b, a] = raw
+
         def load_tab(a):
             nc.sync.dma_start(tab_w[a][:], tab_words[a].rearrange("p n i -> p (n i)").bitcast(I32))
 
@@ -72,24 +85,17 @@ def tile_list_blade_noise_page_kernel(tc, tab_words, tab_scales, offs, w1, w4_wo
         for q in range(4):
             nc.sync.dma_start(tab_s[32 * q : 32 * q + 4, :, :].bitcast(I32),
                               tab_scales[:, 4 * q : 4 * q + 4, :].rearrange("a r n -> r a n").bitcast(I32))
-        load_tab(1)
+        load_w1_pass(0, 0)
         for q in range(4):
             nc.sync.dma_start(w4_s[32 * q : 32 * q + 4, :, :].bitcast(I32),
                               w4_scales[:, 4 * q : 4 * q + 4, :].rearrange("a r n -> r a n").bitcast(I32))
 
-        w1_raw = {}
-
-        def load_w1(b):
-            for a in range(2):
-                raw = big.tile([P, 4, 512], F32, name="w1_raw", tag="big", align_bytes=64)
-                nc.sync.dma_start(raw[:], w1[512 * a : 512 * (a + 1), 512 * b : 512 * (b + 1)].rearrange("(p j) c -> p j c", j=4))
-                w1_raw[b, a] = raw
-
-        load_w1(0)
+        load_tab(1)
+        load_w1_pass(0, 1)
         load_w4(1)
         amp_rows = amp.rearrange("(b p t) j -> b t p j", b=2, t=4)
         page_rows = page0.rearrange("(b p t) m -> b t p m", b=2, t=4)
-        amp_t = [keep.tile([P, S], F32, name="amp%d" % n) for n in range(8)]
+        amp_t = [keep.tile([P, S], F32, name="amp%d" % n) for n in range(9)]
         page = [keep.tile([P, T2], F32, name="page%d" % n) for n in range(8)]
         base_t = [keep.tile([P, 4, PX], F32, name="base%d" % b) for b in range(2)]
 
@@ -105,7 +111,8 @@ def tile_list_blade_noise_page_kernel(tc, tab_words, tab_scales, offs, w1, w4_wo
             if n == 1:
                 nc.sync.dma_start(base_t[0][:], base[0:512, :].rearrange("(p t) j -> p t j", t=4))
             if n == 2:
-                load_w1(1)
+                load_w1_pass(1, 0)
+                load_w1_pass(1, 1)
             if n == 4:
                 nc.sync.dma_start(base_t[1][:], base[512:1024, :].rearrange("(p t) j -> p t j", t=4))
 
@@ -147,37 +154,45 @@ def tile_list_blade_noise_page_kernel(tc, tab_words, tab_scales, offs, w1, w4_wo
             nc.vector.quantize_mx(out=w1_c[:, b, a, :].bitcast(FP8X4), scales=w1_s[:, b, a, :],
                                   in_=w1_g[b, a][:].rearrange("p t q j -> p (t q j)"))
 
-        work = [keep.tile([P, S], F32, name="work%d" % n) for n in range(8)]
+        work = [keep.tile([P, S], F32, name="work%d" % n, tag="work%d" % n, align_bytes=64) for n in range(8)]
+
+        def parts(n):
+            return [slice(0, 256), slice(256, 512)] if n == 0 else [slice(0, 512)]
 
         def phase(n):
             b, t = divmod(n, 4)
-            acc = psum.tile([P, S], F32, name="acc_b", tag="acc_b", bufs=3)
+            acc = psum.tile([P, S], F32, name="acc_b", tag="acc_b", bufs=NB)
             for a in range(2):
                 nc.tensor.matmul_mx(acc[:], lhsT=w4_wd[b][:, a, t, :].bitcast(FP4X4), lhsT_scale=w4_sd[b][:, a, t, :],
                                     rhs=v_w[:, a, :].bitcast(FP8X4), rhs_scale=v_s[:, a, :], start=(a == 0), stop=(a == 1))
             turns = ring.tile([P, S], U32, name="turns")
-            nc.scalar.activation(turns[:], acc[:], ACT.Copy, bias=ROUNDER, scale=1.0 / TWO_PI)
             whole = ring.tile([P, S], F32, name="whole")
-            nc.scalar.activation(whole[:], turns[:], ACT.Copy, bias=-ROUNDER, scale=1.0)
-            nc.vector.scalar_tensor_tensor(work[n][:], whole[:], -TWO_PI, acc[:], ALU.mult, ALU.add)
+            for js in parts(n):
+                nc.scalar.activation(turns[:, js], acc[:, js], ACT.Copy, bias=ROUNDER, scale=1.0 / TWO_PI)
+            for js in parts(n):
+                nc.scalar.activation(whole[:, js], turns[:, js], ACT.Copy, bias=-ROUNDER, scale=1.0)
+            for js in parts(n):
+                nc.vector.scalar_tensor_tensor(work[n][:, js], whole[:, js], -TWO_PI, acc[:, js], ALU.mult, ALU.add)
 
         def sine(n):
-            nc.scalar.activation(work[n][:], work[n][:], ACT.Sin)
+            for js in parts(n):
+                nc.scalar.activation(work[n][:, js], work[n][:, js], ACT.Sin)
 
         def pre_amp(n):
             b, t = divmod(n, 4)
-            nc.gpsimd.tensor_scalar(amp_t[n][:], amp_t[n][:], gain_c[:, b, t : t + 1], 0.0, ALU.mult, ALU.add)
+            if USE_POOL and n > 0:
+                nc.gpsimd.tensor_scalar(amp_t[n][:], amp_t[n][:], gain_c[:, b, t : t + 1], 0.0, ALU.mult, ALU.add)
 
         def times_amp(n):
             b, t = divmod(n, 4)
-            if USE_POOL:
+            if USE_POOL and n > 0:
                 nc.gpsimd.tensor_tensor(work[n][:], work[n][:], amp_t[n][:], ALU.mult)
             else:
                 nc.vector.scalar_tensor_tensor(work[n][:], work[n][:], gain_c[:, b, t : t + 1], amp_t[n][:], ALU.mult, ALU.mult)
 
         def direct(n):
             b, t = divmod(n, 4)
-            acc = psum.tile([P, S], F32, name="acc_a", tag="acc_a", bufs=2)
+            acc = psum.tile([P, S], F32, name="acc_a", tag="acc_a", bufs=8 - NB)
             cols = slice(P * t, P * (t + 1))
             for a in range(2):
                 nc.tensor.matmul_mx(acc[:], lhsT=w1_c[:, b, a, cols].bitcast(FP8X4), lhsT_scale=w1_s[:, b, a, cols],
@@ -188,17 +203,19 @@ def tile_list_blade_noise_page_kernel(tc, tab_words, tab_scales, offs, w1, w4_wo
             return wgs_first[:] if t == 0 else wgs_rest[:, t - 1, :]
 
         def times_wgs(n):
-            nc.gpsimd.tensor_tensor(work[n][:], work[n][:], wgs_of(n % 4), ALU.mult)
+            if USE_POOL and n > 0:
+                nc.gpsimd.tensor_tensor(amp_t[n + 1 if n else 8][:], work[n][:], wgs_of(n % 4), ALU.mult)
 
         picked = {}
 
         def put_and_pick(n):
-            if USE_POOL:
-                nc.vector.tensor_copy(page[n][:].indirect(list2[:]), work[n][:])
+            if USE_POOL and n > 0:
+                nc.vector.tensor_copy(page[n][:].indirect(list2[:]), amp_t[n + 1 if n else 8][:])
             else:
                 nc.vector.tensor_tensor(page[n][:].indirect(list2[:]), work[n][:], wgs_of(n % 4), ALU.mult)
-            g = work[n]
-            nc.vector.tensor_copy(g[:], page[n][:].indirect(list3[:]))
+            g = amp_t[n]
+            if n < 7:
+                nc.vector.tensor_copy(g[:], page[n][:].indirect(list3[:]))
             picked[n] = g
 
         page_pairs = {}
@@ -216,17 +233,17 @@ def tile_list_blade_noise_page_kernel(tc, tab_words, tab_scales, offs, w1, w4_wo
         def plus_base(n):
             b, t = divmod(n, 4)
             eng = nc.gpsimd if USE_POOL else nc.vector
-            eng.tensor_tensor(picked[n][:], picked[n][:], base_t[b][:, t, :], ALU.add)
+            eng.tensor_tensor(work[n + YLAG][:], picked[n][:], base_t[b][:, t, :], ALU.add)
 
         def round_x(n):
             b, t = divmod(n, 4)
             if t == 0:
                 x_pairs[b] = mid.tile([P, 2, PX, 2], BF16, name="x_pairs", tag="mid", align_bytes=64)
-            nc.scalar.activation(x_pairs[b][:, t // 2, :, t % 2], picked[n][:], ACT.Copy, scale=qv_c[:, b, t : t + 1])
+            nc.scalar.activation(x_pairs[b][:, t // 2, :, t % 2], work[n + YLAG][:], ACT.Copy, scale=qv_c[:, b, t : t + 1])
 
-        page_c = keep.tile([P, 2, T2], U32, name="page_c", align_bytes=64)
+        page_c = {1: keep.tile([P, T2], U32, name="page_c1", align_bytes=64)}
         page_s = keep.tile([P, 2, T2], U8, name="page_s", align_bytes=64)
-        x_c = keep.tile([P, 2, PX], U32, name="x_c", align_bytes=64)
+        x_c = {1: keep.tile([P, PX], U32, name="x_c1", align_bytes=64)}
         x_s = keep.tile([P, 2, PX], U8, name="x_s", align_bytes=64)
 
         def weave(dst, src, on_vector):
@@ -250,11 +267,13 @@ def tile_list_blade_noise_page_kernel(tc, tab_words, tab_scales, offs, w1, w4_wo
             woven["x", b] = g
 
         def quant_page(b):
-            nc.vector.quantize_mx(out=page_c[:, b, :].bitcast(FP8X4), scales=page_s[:, b, :],
+            page_c[b] = keep.tile([P, T2], U32, name="page_c0", tag="work%d" % HOLD_P, align_bytes=64)
+            nc.vector.quantize_mx(out=page_c[b][:].bitcast(FP8X4), scales=page_s[:, b, :],
                                   in_=woven["p", b][:].rearrange("p c t -> p (c t)"))
 
         def quant_x(b):
-            nc.vector.quantize_mx(out=x_c[:, b, :].bitcast(FP8X4), scales=x_s[:, b, :],
+            x_c[b] = keep.tile([P, PX], U32, name="x_c0", tag="work%d" % HOLD_X, align_bytes=64)
+            nc.vector.quantize_mx(out=x_c[b][:].bitcast(FP8X4), scales=x_s[:, b, :],
                                   in_=woven["x", b][:].rearrange("p c t -> p (c t)"))
 
         def scale_base(t):
@@ -262,68 +281,94 @@ def tile_list_blade_noise_page_kernel(tc, tab_words, tab_scales, offs, w1, w4_wo
 
         def finish_x(n):
             b, t = divmod(n, 4)
-            nc.vector.scalar_tensor_tensor(x_pairs[b][:, t // 2, :, t % 2], work[n][:], qv_c[:, b, t : t + 1], base_t[b][:, t, :], ALU.mult, ALU.add)
+            nc.vector.scalar_tensor_tensor(x_pairs[b][:, t // 2, :, t % 2], picked[n][:], qv_c[:, b, t : t + 1], base_t[b][:, t, :], ALU.mult, ALU.add)
 
         def last_tile():
             b, t, n = 1, 3, 7
             g = big.tile([P, T2, 4], BF16, name="page_g", tag="big", align_bytes=64)
             words = page_pairs[b][:].rearrange("p u c e -> p u (c e)").bitcast(F32).rearrange("p u c -> p c u")
-            nc.vector.scalar_tensor_tensor(work[n][:], work[n][:], -1.0, work[n][:], ALU.mult, ALU.max)
-            finish_x(n)
-            weave_x(b, True)
-            for half in range(2):
+            gx = mid.tile([P, PX, 4], BF16, name="x_g", tag="mid", align_bytes=64)
+            x_words = x_pairs[b][:].rearrange("p u c e -> p u (c e)").bitcast(F32).rearrange("p u c -> p c u")
+            halves = [slice(256 * half, 256 * (half + 1)) for half in range(2)]
+            col = amp_t[n]
+            for half, js in enumerate(halves):
+                nc.vector.tensor_copy(col[:, js], page[n][:].indirect(list3[:, 16 * half : 16 * (half + 1)]))
+            for js in halves:
+                nc.vector.scalar_tensor_tensor(col[:, js], col[:, js], -1.0, col[:, js], ALU.mult, ALU.max)
+            for js in halves:
+                nc.vector.scalar_tensor_tensor(x_pairs[b][:, 1, js, 1], col[:, js], qv_c[:, b, t : t + 1], base_t[b][:, t, js], ALU.mult, ALU.add)
+            for js in halves:
+                nc.vector.tensor_copy(gx[:].bitcast(F32)[:, js, :], x_words[:, js, :])
+            for half, js in enumerate(halves):
                 cols = slice(512 * half, 512 * (half + 1))
                 nc.scalar.copy(page_pairs[b][:, 1, cols, 1], page[n][:, cols])
                 nc.scalar.copy(g[:].bitcast(F32)[:, cols, :], words[:, cols, :])
-                if half == 1:
-                    quant_x(b)
-                nc.vector.quantize_mx(out=page_c[:, b, cols].bitcast(FP8X4), scales=page_s[:, b, cols],
+                nc.vector.quantize_mx(out=x_c[b][:, js].bitcast(FP8X4), scales=x_s[:, b, js],
+                                      in_=gx[:, js, :].rearrange("p c t -> p (c t)"))
+            for half in range(2):
+                cols = slice(512 * half, 512 * (half + 1))
+                nc.vector.quantize_mx(out=page_c[b][:, cols].bitcast(FP8X4), scales=page_s[:, b, cols],
                                       in_=g[:, cols, :].rearrange("p c t -> p (c t)"))
 
-        deal_w4(0)
-        phase(0)
-        phase(1)
-        sine(0)
-        weave_w1(0, 0, False)
-        weave_w1(0, 1, True)
-        quant_w1(0, 0)
-        quant_w1(0, 1)
-        deal_w4(1)
-        for n in range(8):
-            times_amp(n)
-            direct(n)
-            put_and_pick(n)
-            if n + 1 < 8:
-                sine(n + 1)
-            if n + 2 < 8:
-                phase(n + 2)
-            if n in (1, 2):
-                weave_w1(1, n - 1, False)
-                quant_w1(1, n - 1)
-            if n in (4, 5):
-                scale_base(n - 2)
-            if n < 7:
-                round_page(n)
-                magnitude(n)
+        def after(n):
+            round_page(n)
+            magnitude(n)
             if n < 6:
                 plus_base(n)
                 round_x(n)
-            if n == 6:
+            else:
                 finish_x(n)
             if n == 3:
                 weave_page(0, False)
                 weave_x(0, False)
+            if n == HOLD_P - YLAG:
                 quant_page(0)
+            if n == HOLD_X - YLAG:
                 quant_x(0)
+
+        deal_w4(0)
+        weave_w1(0, 0, False)
+        phase(0)
+        sine(0)
+        weave_w1(0, 1, True)
+        quant_w1(0, 0)
+        quant_w1(0, 1)
+        times_amp(0)
+        direct(0)
+        put_and_pick(0)
+        deal_w4(1)
+        for n in range(1, AHEAD):
+            phase(n)
+        for n in range(8):
+            if n + 1 < 8:
+                sine(n + 1)
+                pre_amp(n + 1)
+                times_amp(n + 1)
+            times_wgs(n)
+            if n + AHEAD < 8:
+                phase(n + AHEAD)
+            if n + 1 < 8:
+                direct(n + 1)
+            if n > 0:
+                put_and_pick(n)
+            if n in (0, 1):
+                weave_w1(1, n, False)
+                quant_w1(1, n)
+            if n in (4, 5):
+                scale_base(n - 2)
+            if n >= LAG:
+                after(n - LAG)
+        for n in range(8 - LAG, 7):
+            after(n)
         last_tile()
 
         for c in range(8):
-            tag, bufs = (("acc_o", 3), ("acc_b", 3), ("acc_a", 2))[c // 3]
+            tag, bufs = ("acc_b", NB) if c < NB else ("acc_a", 8 - NB)
             acc = psum.tile([P, PX], F32, name="acc_o", tag=tag, bufs=bufs)
             cols = slice(P * c, P * (c + 1))
             for b in range(2):
-                nc.tensor.matmul_mx(acc[:], lhsT=page_c[:, b, cols].bitcast(FP8X4), lhsT_scale=page_s[:, b, cols],
-                                    rhs=x_c[:, b, :].bitcast(FP8X4), rhs_scale=x_s[:, b, :], start=(b == 0), stop=(b == 1))
+                nc.tensor.matmul_mx(acc[:], lhsT=page_c[b][:, cols].bitcast(FP8X4), lhsT_scale=page_s[:, b, cols],
+                                    rhs=x_c[b][:].bitcast(FP8X4), rhs_scale=x_s[:, b, :], start=(b == 0), stop=(b == 1))
             res = amp_t[c]
             nc.vector.tensor_scalar(res[:], acc[:], slot_c[:, c : c + 1], None, ALU.max)
             nc.sync.dma_start(out[cols, :], res[:])

@@ -2,6 +2,7 @@ import math
 from contextlib import ExitStack
 
 import concourse.mybir as mybir
+from concourse.masks import make_identity
 
 K, T, S, H, T2, PX = 1024, 2048, 512, 1024, 1024, 512
 FLOPS = 2 * K * H * S * 2 + 2 * H * T2 * PX
@@ -20,13 +21,17 @@ ACT = mybir.ActivationFunctionType
 P = 128
 ROUNDER = 12582912.0
 TWO_PI = 2.0 * math.pi
-USE_POOL = True
-NB = 4
-AHEAD = 4
-LAG = 2
-YLAG = 2
-HOLD_P = 6
-HOLD_X = 7
+NEG_V = False
+LAG = 1
+ANG_AT = 0
+W0_V = True
+EARLY_W1 = False
+W1_AT = 1
+HOLD_P = 5
+HOLD_X = 6
+VQ = 0
+XW_V = False
+GROUPS = ((0,), (1,), (2, 3), (4, 5), (6, 7))
 
 
 def tile_list_blade_noise_page_kernel(tc, tab_words, tab_scales, offs, w1, w4_words, w4_scales, amp, gain,
@@ -36,7 +41,6 @@ def tile_list_blade_noise_page_kernel(tc, tab_words, tab_scales, offs, w1, w4_wo
         keep = ctx.enter_context(tc.tile_pool(name="keep", bufs=1))
         big = ctx.enter_context(tc.tile_pool(name="big", bufs=6))
         mid = ctx.enter_context(tc.tile_pool(name="mid", bufs=4))
-        ring = ctx.enter_context(tc.tile_pool(name="ring", bufs=3))
         psum = ctx.enter_context(tc.psum_pool(name="psum", bufs=1))
 
         warm = keep.tile([P, 1], F32, name="warm")
@@ -47,6 +51,8 @@ def tile_list_blade_noise_page_kernel(tc, tab_words, tab_scales, offs, w1, w4_wo
         w4_s = keep.tile([P, 2, H], U8, name="w4_s", align_bytes=64)
         nc.vector.memset(tab_s[:].rearrange("p a n -> p (a n)").bitcast(I32), 0)
         nc.gpsimd.memset(w4_s[:].rearrange("p a n -> p (a n)").bitcast(I32), 0)
+        ident = keep.tile([P, P], F32, name="ident")
+        make_identity(nc, ident[:])
 
         list1 = keep.tile([P, S // 16], U16, name="list1")
         list2 = keep.tile([P, S // 16], U16, name="list2")
@@ -59,13 +65,12 @@ def tile_list_blade_noise_page_kernel(tc, tab_words, tab_scales, offs, w1, w4_wo
         wgs_rows = wgs.rearrange("(p t) j -> p t j", t=4)
         tab_w = [big.tile([P, T], I32, name="tab_w", tag="big", align_bytes=64) for a in range(2)]
         w4_w = [keep.tile([P, 2, H], U8, name="w4_w%d" % b, align_bytes=64) for b in range(2)]
+        w1_raw = {}
 
         def load_w4(b):
             nc.sync.dma_start(w4_w[b][:].bitcast(I32), w4_words[:, :, H * b : H * (b + 1)].rearrange("a p n -> p a n").bitcast(I32))
 
-        w1_raw = {}
-
-        def load_w1_pass(b, a):
+        def load_w1(b, a):
             raw = big.tile([P, 4, 512], F32, name="w1_raw", tag="big", align_bytes=64)
             nc.sync.dma_start(raw[:], w1[512 * a : 512 * (a + 1), 512 * b : 512 * (b + 1)].rearrange("(p j) c -> p j c", j=4))
             w1_raw[b, a] = raw
@@ -73,51 +78,52 @@ def tile_list_blade_noise_page_kernel(tc, tab_words, tab_scales, offs, w1, w4_wo
         def load_tab(a):
             nc.sync.dma_start(tab_w[a][:], tab_words[a].rearrange("p n i -> p (n i)").bitcast(I32))
 
+        def load_scales(tile, rows):
+            for q in range(4):
+                nc.sync.dma_start(tile[32 * q : 32 * q + 4, :, :].bitcast(I32),
+                                  rows[:, 4 * q : 4 * q + 4, :].rearrange("a r n -> r a n").bitcast(I32))
+
         nc.sync.dma_start(list1[:], offs)
         nc.sync.dma_start(list2[:], offs2)
         nc.sync.dma_start(list3[:], offs3)
         nc.sync.dma_start(gain_c[:], gain.rearrange("(b p t) -> p b t", b=2, t=4))
         nc.sync.dma_start(qv_c[:], qv.rearrange("(b p t) -> p b t", b=2, t=4))
-        load_w4(0)
         load_tab(0)
-        for q in range(1):
+        for q in range(2):
             nc.sync.dma_start(wgs_first[32 * q : 32 * (q + 1), :], wgs_rows[:, 0, :])
-        for q in range(4):
-            nc.sync.dma_start(tab_s[32 * q : 32 * q + 4, :, :].bitcast(I32),
-                              tab_scales[:, 4 * q : 4 * q + 4, :].rearrange("a r n -> r a n").bitcast(I32))
-        load_w1_pass(0, 0)
-        for q in range(4):
-            nc.sync.dma_start(w4_s[32 * q : 32 * q + 4, :, :].bitcast(I32),
-                              w4_scales[:, 4 * q : 4 * q + 4, :].rearrange("a r n -> r a n").bitcast(I32))
-
+        load_scales(tab_s, tab_scales)
+        if EARLY_W1:
+            load_w1(0, 0)
         load_tab(1)
-        load_w1_pass(0, 1)
-        load_w4(1)
+        load_w4(0)
+        load_scales(w4_s, w4_scales)
+        if not EARLY_W1:
+            load_w1(0, 0)
+        load_w1(0, 1)
+
         amp_rows = amp.rearrange("(b p t) j -> b t p j", b=2, t=4)
         page_rows = page0.rearrange("(b p t) m -> b t p m", b=2, t=4)
-        amp_t = [keep.tile([P, S], F32, name="amp%d" % n) for n in range(9)]
+        amp_t = [keep.tile([P, S], F32, name="amp%d" % n) for n in range(8)]
         page = [keep.tile([P, T2], F32, name="page%d" % n) for n in range(8)]
         base_t = [keep.tile([P, 4, PX], F32, name="base%d" % b) for b in range(2)]
 
-        def load_tile(n):
+        for n in range(8):
             nc.sync.dma_start(amp_t[n][:], amp_rows[n // 4, n % 4])
             if n == 0:
-                for q in range(1, 4):
+                for q in range(2, 4):
                     nc.sync.dma_start(wgs_first[32 * q : 32 * (q + 1), :], wgs_rows[:, 0, :])
             if n == 1:
                 for q in range(4):
                     nc.sync.dma_start(wgs_rest[32 * q : 32 * (q + 1), :, :], wgs_rows[:, 1:4, :])
             nc.sync.dma_start(page[n][:], page_rows[n // 4, n % 4])
             if n == 1:
+                load_w4(1)
                 nc.sync.dma_start(base_t[0][:], base[0:512, :].rearrange("(p t) j -> p t j", t=4))
             if n == 2:
-                load_w1_pass(1, 0)
-                load_w1_pass(1, 1)
+                load_w1(1, 0)
+                load_w1(1, 1)
             if n == 4:
                 nc.sync.dma_start(base_t[1][:], base[512:1024, :].rearrange("(p t) j -> p t j", t=4))
-
-        for n in range(8):
-            load_tile(n)
         with nc.allow_non_contiguous_dma(reason="one value a partition"):
             nc.sync.dma_start(slot_c[:], slot.rearrange("(c p) -> p c", p=P))
 
@@ -128,21 +134,14 @@ def tile_list_blade_noise_page_kernel(tc, tab_words, tab_scales, offs, w1, w4_wo
             nc.vector.tensor_copy(v_s[:, a, :], tab_s[:, a, :].indirect(list1[:]))
         nc.vector.tensor_copy(v_w[:, 1, :], tab_w[1][:].bitcast(U32).indirect(list1[:]))
 
-        w4_wd = [keep.tile([P, 2, 4, 256], U8, name="w4_wd%d" % b, align_bytes=64) for b in range(2)]
-        w4_sd = [keep.tile([P, 2, 4, P], U8, name="w4_sd%d" % b, align_bytes=64) for b in range(2)]
-
-        def deal_w4(b):
-            nc.vector.tensor_copy(w4_wd[b][:].bitcast(U16), w4_w[b][:].bitcast(U16).rearrange("p a (q t) -> p a t q", t=4))
-            nc.vector.tensor_copy(w4_sd[b][:], w4_s[:, :, 512 * b : 512 * (b + 1)].rearrange("p a (q t) -> p a t q", t=4))
-
         w1_c = keep.tile([P, 2, 2, 512], U32, name="w1_c", align_bytes=64)
         w1_s = keep.tile([P, 2, 2, 512], U8, name="w1_s", align_bytes=64)
         w1_g = {}
 
         def weave_w1(b, a, on_vector):
             g = mid.tile([P, 4, P, 4], BF16, name="w1_g", tag="mid", align_bytes=64)
-            dst = g[:].rearrange("p t q j -> p q j t")
-            src = w1_raw[b, a][:].rearrange("p j (q t) -> p q j t", t=4)
+            dst = g[:].rearrange("p t q j -> p q t j")
+            src = w1_raw[b, a][:].rearrange("p j (q t) -> p q t j", t=4)
             if on_vector:
                 nc.vector.tensor_copy(dst, src)
             else:
@@ -155,140 +154,130 @@ def tile_list_blade_noise_page_kernel(tc, tab_words, tab_scales, offs, w1, w4_wo
                                   in_=w1_g[b, a][:].rearrange("p t q j -> p (t q j)"))
 
         work = [keep.tile([P, S], F32, name="work%d" % n, tag="work%d" % n, align_bytes=64) for n in range(8)]
+        angle = {}
+        turns = {}
+        shifted = {}
+        minus_whole = {}
 
-        def parts(n):
-            return [slice(0, 256), slice(256, 512)] if n == 0 else [slice(0, 512)]
+        def angles(b):
+            turns[b] = keep.tile([P, 4, 4, P], F32, name="turns", tag="turns")
+            shifted[b] = keep.tile([P, 4, 4, P], U32, name="shifted", tag="shifted")
+            minus_whole[b] = keep.tile([P, 4, 4, P], F32, name="minus_whole", tag="minus_whole")
+            for c in range(4):
+                acc = psum.tile([P, 512], F32, name="angle", tag="angle", bufs=4)
+                js = slice(P * c, P * (c + 1))
+                for a in range(2):
+                    nc.tensor.matmul_mx(acc[:], lhsT=v_w[:, a, js].bitcast(FP8X4), lhsT_scale=v_s[:, a, js],
+                                        rhs=w4_w[b][:, a, :].bitcast(FP4X4), rhs_scale=w4_s[:, a, 512 * b : 512 * (b + 1)],
+                                        start=(a == 0), stop=(a == 1))
+                angle[b, c] = acc
 
-        def phase(n):
-            b, t = divmod(n, 4)
-            acc = psum.tile([P, S], F32, name="acc_b", tag="acc_b", bufs=NB)
-            for a in range(2):
-                nc.tensor.matmul_mx(acc[:], lhsT=w4_wd[b][:, a, t, :].bitcast(FP4X4), lhsT_scale=w4_sd[b][:, a, t, :],
-                                    rhs=v_w[:, a, :].bitcast(FP8X4), rhs_scale=v_s[:, a, :], start=(a == 0), stop=(a == 1))
-            turns = ring.tile([P, S], U32, name="turns")
-            whole = ring.tile([P, S], F32, name="whole")
-            for js in parts(n):
-                nc.scalar.activation(turns[:, js], acc[:, js], ACT.Copy, bias=ROUNDER, scale=1.0 / TWO_PI)
-            for js in parts(n):
-                nc.scalar.activation(whole[:, js], turns[:, js], ACT.Copy, bias=-ROUNDER, scale=1.0)
-            for js in parts(n):
-                nc.vector.scalar_tensor_tensor(work[n][:, js], whole[:, js], -TWO_PI, acc[:, js], ALU.mult, ALU.add)
+        def read_angles(b, ts, blocks, on_vector):
+            for c in blocks:
+                src = angle[b, c][:].rearrange("j (q t) -> j t q", t=4)[:, ts, :]
+                nc.scalar.activation(shifted[b][:, ts, c, :], src, ACT.Copy, bias=ROUNDER, scale=1.0 / TWO_PI)
+                if on_vector:
+                    nc.vector.tensor_scalar(turns[b][:, ts, c, :], src, 1.0 / TWO_PI, None, ALU.mult)
+                else:
+                    nc.scalar.activation(turns[b][:, ts, c, :], src, ACT.Copy, scale=1.0 / TWO_PI)
 
-        def sine(n):
-            for js in parts(n):
-                nc.scalar.activation(work[n][:, js], work[n][:, js], ACT.Sin)
-
-        def pre_amp(n):
-            b, t = divmod(n, 4)
-            if USE_POOL and n > 0:
-                nc.gpsimd.tensor_scalar(amp_t[n][:], amp_t[n][:], gain_c[:, b, t : t + 1], 0.0, ALU.mult, ALU.add)
+        def sines(group):
+            rest = {}
+            for n in group:
+                b, t = divmod(n, 4)
+                if NEG_V:
+                    nc.vector.tensor_scalar(minus_whole[b][:, t], shifted[b][:, t].bitcast(I32), -1.0, ROUNDER, ALU.mult, ALU.add)
+                else:
+                    nc.scalar.activation(minus_whole[b][:, t], shifted[b][:, t], ACT.Copy, bias=ROUNDER, scale=-1.0)
+                rest[n] = psum.tile([P, S], F32, name="rest", tag="rest", bufs=2)
+            for c in range(4):
+                js = slice(P * c, P * (c + 1))
+                for n in group:
+                    b, t = divmod(n, 4)
+                    nc.tensor.matmul(rest[n][:, js], lhsT=turns[b][:, t, c, :], rhs=ident[:], is_transpose=True, start=True, stop=False)
+                    nc.tensor.matmul(rest[n][:, js], lhsT=minus_whole[b][:, t, c, :], rhs=ident[:], is_transpose=True, start=False, stop=True)
+            for n in group:
+                nc.scalar.activation(work[n][:], rest[n][:], ACT.Sin, scale=TWO_PI)
 
         def times_amp(n):
             b, t = divmod(n, 4)
-            if USE_POOL and n > 0:
-                nc.gpsimd.tensor_tensor(work[n][:], work[n][:], amp_t[n][:], ALU.mult)
-            else:
-                nc.vector.scalar_tensor_tensor(work[n][:], work[n][:], gain_c[:, b, t : t + 1], amp_t[n][:], ALU.mult, ALU.mult)
+            nc.vector.scalar_tensor_tensor(work[n][:], work[n][:], gain_c[:, b, t : t + 1], amp_t[n][:], ALU.mult, ALU.mult)
 
         def direct(n):
             b, t = divmod(n, 4)
-            acc = psum.tile([P, S], F32, name="acc_a", tag="acc_a", bufs=8 - NB)
+            acc = psum.tile([P, S], F32, name="acc_a", tag="acc_a", bufs=2)
             cols = slice(P * t, P * (t + 1))
             for a in range(2):
                 nc.tensor.matmul_mx(acc[:], lhsT=w1_c[:, b, a, cols].bitcast(FP8X4), lhsT_scale=w1_s[:, b, a, cols],
                                     rhs=v_w[:, a, :].bitcast(FP8X4), rhs_scale=v_s[:, a, :], start=(a == 0), stop=(a == 1))
             nc.vector.scalar_tensor_tensor(work[n][:], acc[:], gain_c[:, b, t : t + 1], work[n][:], ALU.mult, ALU.add)
 
-        def wgs_of(t):
-            return wgs_first[:] if t == 0 else wgs_rest[:, t - 1, :]
+        def put(n):
+            t = n % 4
+            factor = wgs_first[:] if t == 0 else wgs_rest[:, t - 1, :]
+            nc.vector.tensor_tensor(page[n][:].indirect(list2[:]), work[n][:], factor, ALU.mult)
 
-        def times_wgs(n):
-            if USE_POOL and n > 0:
-                nc.gpsimd.tensor_tensor(amp_t[n + 1 if n else 8][:], work[n][:], wgs_of(n % 4), ALU.mult)
+        def pick(n):
+            nc.vector.tensor_copy(amp_t[n][:], page[n][:].indirect(list3[:]))
 
-        picked = {}
-
-        def put_and_pick(n):
-            if USE_POOL and n > 0:
-                nc.vector.tensor_copy(page[n][:].indirect(list2[:]), amp_t[n + 1 if n else 8][:])
-            else:
-                nc.vector.tensor_tensor(page[n][:].indirect(list2[:]), work[n][:], wgs_of(n % 4), ALU.mult)
-            g = amp_t[n]
-            if n < 7:
-                nc.vector.tensor_copy(g[:], page[n][:].indirect(list3[:]))
-            picked[n] = g
-
-        page_pairs = {}
-        x_pairs = {}
+        page_rounded = {}
+        x_rounded = {}
 
         def round_page(n):
             b, t = divmod(n, 4)
             if t == 0:
-                page_pairs[b] = big.tile([P, 2, T2, 2], BF16, name="page_pairs", tag="big", align_bytes=64)
-            nc.scalar.copy(page_pairs[b][:, t // 2, :, t % 2], page[n][:])
+                page_rounded[b] = big.tile([P, 4, T2], BF16, name="page_rounded", tag="big", align_bytes=64)
+            nc.scalar.copy(page_rounded[b][:, t, :], page[n][:])
 
         def magnitude(n):
-            nc.scalar.activation(picked[n][:], picked[n][:], ACT.Abs)
-
-        def plus_base(n):
-            b, t = divmod(n, 4)
-            eng = nc.gpsimd if USE_POOL else nc.vector
-            eng.tensor_tensor(work[n + YLAG][:], picked[n][:], base_t[b][:, t, :], ALU.add)
-
-        def round_x(n):
-            b, t = divmod(n, 4)
-            if t == 0:
-                x_pairs[b] = mid.tile([P, 2, PX, 2], BF16, name="x_pairs", tag="mid", align_bytes=64)
-            nc.scalar.activation(x_pairs[b][:, t // 2, :, t % 2], work[n + YLAG][:], ACT.Copy, scale=qv_c[:, b, t : t + 1])
+            nc.scalar.activation(amp_t[n][:], amp_t[n][:], ACT.Abs)
 
         page_c = {1: keep.tile([P, T2], U32, name="page_c1", align_bytes=64)}
         page_s = keep.tile([P, 2, T2], U8, name="page_s", align_bytes=64)
         x_c = {1: keep.tile([P, PX], U32, name="x_c1", align_bytes=64)}
         x_s = keep.tile([P, 2, PX], U8, name="x_s", align_bytes=64)
 
-        def weave(dst, src, on_vector):
-            d = dst[:].bitcast(F32)
-            s = src[:].rearrange("p u c e -> p u (c e)").bitcast(F32).rearrange("p u c -> p c u")
+        def weave_cols(dst, src, cols, on_vector):
+            s = src[:, :, cols].rearrange("p t c -> p c t")
             if on_vector:
-                nc.vector.tensor_copy(d, s)
+                nc.vector.tensor_copy(dst[:, cols, :], s)
             else:
-                nc.scalar.copy(d, s)
+                nc.scalar.copy(dst[:, cols, :], s)
 
         woven = {}
 
-        def weave_page(b, on_vector):
-            g = big.tile([P, T2, 4], BF16, name="page_g", tag="big", align_bytes=64)
-            weave(g, page_pairs[b], on_vector)
-            woven["p", b] = g
+        def weave_first_half(k):
+            if k == 0:
+                woven["p"] = big.tile([P, T2, 4], BF16, name="page_g", tag="big", align_bytes=64)
+            if k == 4:
+                woven["x"] = mid.tile([P, PX, 4], BF16, name="x_g", tag="mid", align_bytes=64)
+            if k < 4:
+                weave_cols(woven["p"], page_rounded[0], slice(256 * k, 256 * (k + 1)), False)
+            else:
+                weave_cols(woven["x"], x_rounded[0], slice(256 * (k - 4), 256 * (k - 3)), XW_V)
 
-        def weave_x(b, on_vector):
-            g = mid.tile([P, PX, 4], BF16, name="x_g", tag="mid", align_bytes=64)
-            weave(g, x_pairs[b], on_vector)
-            woven["x", b] = g
+        def quant_page_first():
+            page_c[0] = keep.tile([P, T2], U32, name="page_c0", tag="work%d" % HOLD_P, align_bytes=64)
+            nc.vector.quantize_mx(out=page_c[0][:].bitcast(FP8X4), scales=page_s[:, 0, :], in_=woven["p"][:].rearrange("p c t -> p (c t)"))
 
-        def quant_page(b):
-            page_c[b] = keep.tile([P, T2], U32, name="page_c0", tag="work%d" % HOLD_P, align_bytes=64)
-            nc.vector.quantize_mx(out=page_c[b][:].bitcast(FP8X4), scales=page_s[:, b, :],
-                                  in_=woven["p", b][:].rearrange("p c t -> p (c t)"))
+        def quant_x_first():
+            x_c[0] = keep.tile([P, PX], U32, name="x_c0", tag="work%d" % HOLD_X, align_bytes=64)
+            nc.vector.quantize_mx(out=x_c[0][:].bitcast(FP8X4), scales=x_s[:, 0, :], in_=woven["x"][:].rearrange("p c t -> p (c t)"))
 
-        def quant_x(b):
-            x_c[b] = keep.tile([P, PX], U32, name="x_c0", tag="work%d" % HOLD_X, align_bytes=64)
-            nc.vector.quantize_mx(out=x_c[b][:].bitcast(FP8X4), scales=x_s[:, b, :],
-                                  in_=woven["x", b][:].rearrange("p c t -> p (c t)"))
-
-        def scale_base(t):
-            nc.scalar.activation(base_t[1][:, t, :], base_t[1][:, t, :], ACT.Copy, scale=qv_c[:, 1, t : t + 1])
-
-        def finish_x(n):
+        def scale_base(n):
             b, t = divmod(n, 4)
-            nc.vector.scalar_tensor_tensor(x_pairs[b][:, t // 2, :, t % 2], picked[n][:], qv_c[:, b, t : t + 1], base_t[b][:, t, :], ALU.mult, ALU.add)
+            nc.scalar.activation(base_t[b][:, t, :], base_t[b][:, t, :], ACT.Copy, scale=qv_c[:, b, t : t + 1])
+
+        def finish_x(n, js):
+            b, t = divmod(n, 4)
+            if t == 0:
+                x_rounded[b] = mid.tile([P, 4, PX], BF16, name="x_rounded", tag="mid", align_bytes=64)
+            nc.vector.scalar_tensor_tensor(x_rounded[b][:, t, js], amp_t[n][:, js], qv_c[:, b, t : t + 1], base_t[b][:, t, js], ALU.mult, ALU.add)
 
         def last_tile():
             b, t, n = 1, 3, 7
             g = big.tile([P, T2, 4], BF16, name="page_g", tag="big", align_bytes=64)
-            words = page_pairs[b][:].rearrange("p u c e -> p u (c e)").bitcast(F32).rearrange("p u c -> p c u")
             gx = mid.tile([P, PX, 4], BF16, name="x_g", tag="mid", align_bytes=64)
-            x_words = x_pairs[b][:].rearrange("p u c e -> p u (c e)").bitcast(F32).rearrange("p u c -> p c u")
             halves = [slice(256 * half, 256 * (half + 1)) for half in range(2)]
             col = amp_t[n]
             for half, js in enumerate(halves):
@@ -296,13 +285,14 @@ def tile_list_blade_noise_page_kernel(tc, tab_words, tab_scales, offs, w1, w4_wo
             for js in halves:
                 nc.vector.scalar_tensor_tensor(col[:, js], col[:, js], -1.0, col[:, js], ALU.mult, ALU.max)
             for js in halves:
-                nc.vector.scalar_tensor_tensor(x_pairs[b][:, 1, js, 1], col[:, js], qv_c[:, b, t : t + 1], base_t[b][:, t, js], ALU.mult, ALU.add)
+                finish_x(n, js)
             for js in halves:
-                nc.vector.tensor_copy(gx[:].bitcast(F32)[:, js, :], x_words[:, js, :])
+                weave_cols(gx, x_rounded[b], js, True)
             for half, js in enumerate(halves):
                 cols = slice(512 * half, 512 * (half + 1))
-                nc.scalar.copy(page_pairs[b][:, 1, cols, 1], page[n][:, cols])
-                nc.scalar.copy(g[:].bitcast(F32)[:, cols, :], words[:, cols, :])
+                nc.scalar.copy(page_rounded[b][:, t, cols], page[n][:, cols])
+                for quarter in (2 * half, 2 * half + 1):
+                    weave_cols(g, page_rounded[b], slice(256 * quarter, 256 * (quarter + 1)), quarter >= 4 - VQ)
                 nc.vector.quantize_mx(out=x_c[b][:, js].bitcast(FP8X4), scales=x_s[:, b, js],
                                       in_=gx[:, js, :].rearrange("p c t -> p (c t)"))
             for half in range(2):
@@ -311,59 +301,51 @@ def tile_list_blade_noise_page_kernel(tc, tab_words, tab_scales, offs, w1, w4_wo
                                       in_=g[:, cols, :].rearrange("p c t -> p (c t)"))
 
         def after(n):
-            round_page(n)
+            scale_base(n)
             magnitude(n)
-            if n < 6:
-                plus_base(n)
-                round_x(n)
-            else:
-                finish_x(n)
-            if n == 3:
-                weave_page(0, False)
-                weave_x(0, False)
-            if n == HOLD_P - YLAG:
-                quant_page(0)
-            if n == HOLD_X - YLAG:
-                quant_x(0)
+            finish_x(n, slice(0, PX))
+            round_page(n)
 
-        deal_w4(0)
-        weave_w1(0, 0, False)
-        phase(0)
-        sine(0)
+        weave_w1(0, 0, W0_V)
+        angles(0)
+        read_angles(0, slice(0, 1), range(4), True)
+        sines(GROUPS[0])
         weave_w1(0, 1, True)
         quant_w1(0, 0)
         quant_w1(0, 1)
-        times_amp(0)
-        direct(0)
-        put_and_pick(0)
-        deal_w4(1)
-        for n in range(1, AHEAD):
-            phase(n)
-        for n in range(8):
-            if n + 1 < 8:
-                sine(n + 1)
-                pre_amp(n + 1)
-                times_amp(n + 1)
-            times_wgs(n)
-            if n + AHEAD < 8:
-                phase(n + AHEAD)
-            if n + 1 < 8:
-                direct(n + 1)
-            if n > 0:
-                put_and_pick(n)
-            if n in (0, 1):
-                weave_w1(1, n, False)
-                quant_w1(1, n)
-            if n in (4, 5):
-                scale_base(n - 2)
-            if n >= LAG:
-                after(n - LAG)
-        for n in range(8 - LAG, 7):
-            after(n)
+        read_angles(0, slice(1, 4), range(4), False)
+        for k, group in enumerate(GROUPS):
+            for step in (times_amp, direct, put, pick):
+                for n in group:
+                    if step is not pick or n < 7:
+                        step(n)
+            if k == ANG_AT:
+                angles(1)
+                read_angles(1, slice(0, 4), range(4), False)
+            if k == W1_AT:
+                weave_w1(1, 0, False)
+                quant_w1(1, 0)
+                weave_w1(1, 1, False)
+                quant_w1(1, 1)
+            if k + 1 < len(GROUPS):
+                sines(GROUPS[k + 1])
+            if k >= LAG:
+                for n in GROUPS[k - LAG]:
+                    after(n)
+                if 3 in GROUPS[k - LAG]:
+                    for piece in range(6):
+                        weave_first_half(piece)
+        for group in GROUPS[len(GROUPS) - LAG :]:
+            for n in group:
+                if n < 7:
+                    after(n)
+        scale_base(7)
+        quant_page_first()
+        quant_x_first()
         last_tile()
 
         for c in range(8):
-            tag, bufs = ("acc_b", NB) if c < NB else ("acc_a", 8 - NB)
+            tag, bufs = (("angle", 4), ("angle", 4), ("rest", 2), ("acc_a", 2))[c // 2]
             acc = psum.tile([P, PX], F32, name="acc_o", tag=tag, bufs=bufs)
             cols = slice(P * c, P * (c + 1))
             for b in range(2):

@@ -19,19 +19,11 @@ ALU = mybir.AluOpType
 ACT = mybir.ActivationFunctionType
 
 P = 128
-ROUNDER = 12582912.0
+PASS = 512
+TILES = 8
 TWO_PI = 2.0 * math.pi
-NEG_V = False
-LAG = 1
-ANG_AT = 0
-W0_V = True
-EARLY_W1 = False
-W1_AT = 1
-HOLD_P = 5
-HOLD_X = 6
-VQ = 0
-XW_V = False
-GROUPS = ((0,), (1,), (2, 3), (4, 5), (6, 7))
+ROUNDER = 1.5 * 2.0**23
+WEAVE = 256
 
 
 def tile_list_blade_noise_page_kernel(tc, tab_words, tab_scales, offs, w1, w4_words, w4_scales, amp, gain,
@@ -59,7 +51,7 @@ def tile_list_blade_noise_page_kernel(tc, tab_words, tab_scales, offs, w1, w4_wo
         list3 = keep.tile([P, PX // 16], U16, name="list3")
         gain_c = keep.tile([P, 2, 4], F32, name="gain_c")
         qv_c = keep.tile([P, 2, 4], F32, name="qv_c")
-        slot_c = keep.tile([P, 8], F32, name="slot_c")
+        slot_c = keep.tile([P, T2 // P], F32, name="slot_c")
         wgs_first = keep.tile([P, S], F32, name="wgs_first")
         wgs_rest = keep.tile([P, 3, S], F32, name="wgs_rest")
         wgs_rows = wgs.rearrange("(p t) j -> p t j", t=4)
@@ -68,20 +60,25 @@ def tile_list_blade_noise_page_kernel(tc, tab_words, tab_scales, offs, w1, w4_wo
         w1_raw = {}
 
         def load_w4(b):
-            nc.sync.dma_start(w4_w[b][:].bitcast(I32), w4_words[:, :, H * b : H * (b + 1)].rearrange("a p n -> p a n").bitcast(I32))
+            half = w4_words[:, :, H * b : H * (b + 1)]
+            nc.sync.dma_start(w4_w[b][:].bitcast(I32), half.rearrange("a p n -> p a n").bitcast(I32))
 
         def load_w1(b, a):
-            raw = big.tile([P, 4, 512], F32, name="w1_raw", tag="big", align_bytes=64)
-            nc.sync.dma_start(raw[:], w1[512 * a : 512 * (a + 1), 512 * b : 512 * (b + 1)].rearrange("(p j) c -> p j c", j=4))
-            w1_raw[b, a] = raw
+            w1_raw[b, a] = big.tile([P, 4, PASS], F32, name="w1_raw", tag="big", align_bytes=64)
+            quarter = w1[PASS * a : PASS * (a + 1), PASS * b : PASS * (b + 1)]
+            nc.sync.dma_start(w1_raw[b, a][:], quarter.rearrange("(p i) c -> p i c", i=4))
 
         def load_tab(a):
             nc.sync.dma_start(tab_w[a][:], tab_words[a].rearrange("p n i -> p (n i)").bitcast(I32))
 
         def load_scales(tile, rows):
-            for q in range(4):
-                nc.sync.dma_start(tile[32 * q : 32 * q + 4, :, :].bitcast(I32),
-                                  rows[:, 4 * q : 4 * q + 4, :].rearrange("a r n -> r a n").bitcast(I32))
+            by_u = rows.rearrange("a (q u) n -> u q a n", u=4)
+            for u in range(4):
+                nc.sync.dma_start(tile[u:P:32, :, :].bitcast(I32), by_u[u].bitcast(I32))
+
+        def load_wgs(tile, rows, quarters):
+            for q in quarters:
+                nc.sync.dma_start(tile[32 * q : 32 * (q + 1)], rows)
 
         nc.sync.dma_start(list1[:], offs)
         nc.sync.dma_start(list2[:], offs2)
@@ -89,41 +86,48 @@ def tile_list_blade_noise_page_kernel(tc, tab_words, tab_scales, offs, w1, w4_wo
         nc.sync.dma_start(gain_c[:], gain.rearrange("(b p t) -> p b t", b=2, t=4))
         nc.sync.dma_start(qv_c[:], qv.rearrange("(b p t) -> p b t", b=2, t=4))
         load_tab(0)
-        for q in range(2):
-            nc.sync.dma_start(wgs_first[32 * q : 32 * (q + 1), :], wgs_rows[:, 0, :])
+        load_wgs(wgs_first, wgs_rows[:, 0, :], (0, 1))
         load_scales(tab_s, tab_scales)
-        if EARLY_W1:
-            load_w1(0, 0)
         load_tab(1)
         load_w4(0)
         load_scales(w4_s, w4_scales)
-        if not EARLY_W1:
-            load_w1(0, 0)
+        load_w1(0, 0)
         load_w1(0, 1)
 
         amp_rows = amp.rearrange("(b p t) j -> b t p j", b=2, t=4)
         page_rows = page0.rearrange("(b p t) m -> b t p m", b=2, t=4)
-        amp_t = [keep.tile([P, S], F32, name="amp%d" % n) for n in range(8)]
-        page = [keep.tile([P, T2], F32, name="page%d" % n) for n in range(8)]
+        cols = [keep.tile([P, S], F32, name="cols%d" % n) for n in range(TILES)]
+        page = [keep.tile([P, T2], F32, name="page%d" % n) for n in range(TILES)]
         base_t = [keep.tile([P, 4, PX], F32, name="base%d" % b) for b in range(2)]
 
-        for n in range(8):
-            nc.sync.dma_start(amp_t[n][:], amp_rows[n // 4, n % 4])
-            if n == 0:
-                for q in range(2, 4):
-                    nc.sync.dma_start(wgs_first[32 * q : 32 * (q + 1), :], wgs_rows[:, 0, :])
-            if n == 1:
-                for q in range(4):
-                    nc.sync.dma_start(wgs_rest[32 * q : 32 * (q + 1), :, :], wgs_rows[:, 1:4, :])
-            nc.sync.dma_start(page[n][:], page_rows[n // 4, n % 4])
-            if n == 1:
-                load_w4(1)
-                nc.sync.dma_start(base_t[0][:], base[0:512, :].rearrange("(p t) j -> p t j", t=4))
-            if n == 2:
-                load_w1(1, 0)
-                load_w1(1, 1)
-            if n == 4:
-                nc.sync.dma_start(base_t[1][:], base[512:1024, :].rearrange("(p t) j -> p t j", t=4))
+        def load_amp(*tiles):
+            for n in tiles:
+                nc.sync.dma_start(cols[n][:], amp_rows[n // 4, n % 4])
+
+        def load_page(*tiles):
+            for n in tiles:
+                nc.sync.dma_start(page[n][:], page_rows[n // 4, n % 4])
+
+        def load_base(b):
+            nc.sync.dma_start(base_t[b][:], base[PASS * b : PASS * (b + 1), :].rearrange("(p t) j -> p t j", t=4))
+
+        load_amp(0)
+        load_wgs(wgs_first, wgs_rows[:, 0, :], (2, 3))
+        load_page(0)
+        load_amp(1)
+        load_wgs(wgs_rest, wgs_rows[:, 1:4, :], range(4))
+        load_page(1)
+        load_w4(1)
+        load_amp(2, 3)
+        load_page(2, 3)
+        load_w1(1, 0)
+        load_w1(1, 1)
+        load_base(1)
+        load_base(0)
+        load_page(4, 5)
+        load_amp(4, 5)
+        load_page(6, 7)
+        load_amp(6, 7)
         with nc.allow_non_contiguous_dma(reason="one value a partition"):
             nc.sync.dma_start(slot_c[:], slot.rearrange("(c p) -> p c", p=P))
 
@@ -134,82 +138,86 @@ def tile_list_blade_noise_page_kernel(tc, tab_words, tab_scales, offs, w1, w4_wo
             nc.vector.tensor_copy(v_s[:, a, :], tab_s[:, a, :].indirect(list1[:]))
         nc.vector.tensor_copy(v_w[:, 1, :], tab_w[1][:].bitcast(U32).indirect(list1[:]))
 
-        w1_c = keep.tile([P, 2, 2, 512], U32, name="w1_c", align_bytes=64)
-        w1_s = keep.tile([P, 2, 2, 512], U8, name="w1_s", align_bytes=64)
-        w1_g = {}
+        w1_c = keep.tile([P, 2, 2, PASS], U32, name="w1_c", align_bytes=64)
+        w1_s = keep.tile([P, 2, 2, PASS], U8, name="w1_s", align_bytes=64)
+        w1_woven = {}
 
-        def weave_w1(b, a, on_vector):
-            g = mid.tile([P, 4, P, 4], BF16, name="w1_g", tag="mid", align_bytes=64)
-            dst = g[:].rearrange("p t q j -> p q t j")
-            src = w1_raw[b, a][:].rearrange("p j (q t) -> p q t j", t=4)
-            if on_vector:
+        def weave_w1(b, a):
+            w1_woven[b, a] = mid.tile([P, 4, P, 4], BF16, name="w1_woven", tag="mid", align_bytes=64)
+            dst = w1_woven[b, a][:].rearrange("p t q i -> p q t i")
+            src = w1_raw[b, a][:].rearrange("p i (q t) -> p q t i", t=4)
+            if b == 0:
                 nc.vector.tensor_copy(dst, src)
             else:
-                for half in range(2):
-                    nc.scalar.copy(dst[:, 64 * half : 64 * (half + 1)], src[:, 64 * half : 64 * (half + 1)])
-            w1_g[b, a] = g
+                for q0 in (0, P // 2):
+                    nc.scalar.copy(dst[:, q0 : q0 + P // 2], src[:, q0 : q0 + P // 2])
 
-        def quant_w1(b, a):
+        def quantise_w1(b, a):
             nc.vector.quantize_mx(out=w1_c[:, b, a, :].bitcast(FP8X4), scales=w1_s[:, b, a, :],
-                                  in_=w1_g[b, a][:].rearrange("p t q j -> p (t q j)"))
+                                  in_=w1_woven[b, a][:].rearrange("p t q i -> p (t q i)"))
 
-        work = [keep.tile([P, S], F32, name="work%d" % n, tag="work%d" % n, align_bytes=64) for n in range(8)]
+        work = [keep.tile([P, S], F32, name="work%d" % n, tag="work%d" % n, align_bytes=64) for n in range(TILES)]
         angle = {}
         turns = {}
         shifted = {}
         minus_whole = {}
 
         def angles(b):
-            turns[b] = keep.tile([P, 4, 4, P], F32, name="turns", tag="turns")
-            shifted[b] = keep.tile([P, 4, 4, P], U32, name="shifted", tag="shifted")
+            turns[b] = keep.tile([P, 4, 4, P], F32, name="turns", tag="turns", align_bytes=64)
+            shifted[b] = keep.tile([P, 4, 4, P], U32, name="shifted", tag="shifted", align_bytes=64)
             minus_whole[b] = keep.tile([P, 4, 4, P], F32, name="minus_whole", tag="minus_whole")
             for c in range(4):
-                acc = psum.tile([P, 512], F32, name="angle", tag="angle", bufs=4)
+                angle[b, c] = psum.tile([P, PASS], F32, name="angle", tag="angle", bufs=4)
                 js = slice(P * c, P * (c + 1))
                 for a in range(2):
-                    nc.tensor.matmul_mx(acc[:], lhsT=v_w[:, a, js].bitcast(FP8X4), lhsT_scale=v_s[:, a, js],
-                                        rhs=w4_w[b][:, a, :].bitcast(FP4X4), rhs_scale=w4_s[:, a, 512 * b : 512 * (b + 1)],
+                    nc.tensor.matmul_mx(angle[b, c][:], lhsT=v_w[:, a, js].bitcast(FP8X4), lhsT_scale=v_s[:, a, js],
+                                        rhs=w4_w[b][:, a, :].bitcast(FP4X4),
+                                        rhs_scale=w4_s[:, a, PASS * b : PASS * (b + 1)],
                                         start=(a == 0), stop=(a == 1))
-                angle[b, c] = acc
 
-        def read_angles(b, ts, blocks, on_vector):
-            for c in blocks:
+        def read_angles(b, ts, turns_on_vector):
+            for c in range(4):
                 src = angle[b, c][:].rearrange("j (q t) -> j t q", t=4)[:, ts, :]
                 nc.scalar.activation(shifted[b][:, ts, c, :], src, ACT.Copy, bias=ROUNDER, scale=1.0 / TWO_PI)
-                if on_vector:
+                if turns_on_vector:
                     nc.vector.tensor_scalar(turns[b][:, ts, c, :], src, 1.0 / TWO_PI, None, ALU.mult)
                 else:
                     nc.scalar.activation(turns[b][:, ts, c, :], src, ACT.Copy, scale=1.0 / TWO_PI)
 
-        def sines(group):
+        def sines(*tiles):
             rest = {}
-            for n in group:
+            for n in tiles:
                 b, t = divmod(n, 4)
-                if NEG_V:
-                    nc.vector.tensor_scalar(minus_whole[b][:, t], shifted[b][:, t].bitcast(I32), -1.0, ROUNDER, ALU.mult, ALU.add)
+                if b == 0:
+                    nc.vector.tensor_scalar(minus_whole[b][:, t], shifted[b][:, t].bitcast(I32), -1.0, ROUNDER,
+                                            ALU.mult, ALU.add)
                 else:
                     nc.scalar.activation(minus_whole[b][:, t], shifted[b][:, t], ACT.Copy, bias=ROUNDER, scale=-1.0)
                 rest[n] = psum.tile([P, S], F32, name="rest", tag="rest", bufs=2)
             for c in range(4):
                 js = slice(P * c, P * (c + 1))
-                for n in group:
+                for n in tiles:
                     b, t = divmod(n, 4)
-                    nc.tensor.matmul(rest[n][:, js], lhsT=turns[b][:, t, c, :], rhs=ident[:], is_transpose=True, start=True, stop=False)
-                    nc.tensor.matmul(rest[n][:, js], lhsT=minus_whole[b][:, t, c, :], rhs=ident[:], is_transpose=True, start=False, stop=True)
-            for n in group:
+                    nc.tensor.matmul(rest[n][:, js], lhsT=turns[b][:, t, c, :], rhs=ident[:], is_transpose=True,
+                                     start=True, stop=False)
+                    nc.tensor.matmul(rest[n][:, js], lhsT=minus_whole[b][:, t, c, :], rhs=ident[:], is_transpose=True,
+                                     start=False, stop=True)
+            for n in tiles:
                 nc.scalar.activation(work[n][:], rest[n][:], ACT.Sin, scale=TWO_PI)
 
         def times_amp(n):
             b, t = divmod(n, 4)
-            nc.vector.scalar_tensor_tensor(work[n][:], work[n][:], gain_c[:, b, t : t + 1], amp_t[n][:], ALU.mult, ALU.mult)
+            nc.vector.scalar_tensor_tensor(work[n][:], work[n][:], gain_c[:, b, t : t + 1], cols[n][:],
+                                           ALU.mult, ALU.mult)
 
-        def direct(n):
+        def plus_direct(n):
             b, t = divmod(n, 4)
-            acc = psum.tile([P, S], F32, name="acc_a", tag="acc_a", bufs=2)
-            cols = slice(P * t, P * (t + 1))
+            acc = psum.tile([P, S], F32, name="direct", tag="angle" if b else "sum", bufs=4 if b else 2)
+            rs = slice(P * t, P * (t + 1))
             for a in range(2):
-                nc.tensor.matmul_mx(acc[:], lhsT=w1_c[:, b, a, cols].bitcast(FP8X4), lhsT_scale=w1_s[:, b, a, cols],
-                                    rhs=v_w[:, a, :].bitcast(FP8X4), rhs_scale=v_s[:, a, :], start=(a == 0), stop=(a == 1))
+                nc.tensor.matmul_mx(acc[:], lhsT=w1_c[:, b, a, rs].bitcast(FP8X4), lhsT_scale=w1_s[:, b, a, rs],
+                                    rhs=v_w[:, a, :].bitcast(FP8X4), rhs_scale=v_s[:, a, :],
+                                    start=(a == 0), stop=(a == 1))
             nc.vector.scalar_tensor_tensor(work[n][:], acc[:], gain_c[:, b, t : t + 1], work[n][:], ALU.mult, ALU.add)
 
         def put(n):
@@ -218,139 +226,132 @@ def tile_list_blade_noise_page_kernel(tc, tab_words, tab_scales, offs, w1, w4_wo
             nc.vector.tensor_tensor(page[n][:].indirect(list2[:]), work[n][:], factor, ALU.mult)
 
         def pick(n):
-            nc.vector.tensor_copy(amp_t[n][:], page[n][:].indirect(list3[:]))
+            nc.vector.tensor_copy(cols[n][:], page[n][:].indirect(list3[:]))
+
+        def change_page(*tiles):
+            for step in (times_amp, plus_direct, put, pick):
+                for n in tiles:
+                    step(n)
 
         page_rounded = {}
         x_rounded = {}
 
-        def round_page(n):
+        def round_page(n, ms=slice(0, T2)):
             b, t = divmod(n, 4)
             if t == 0:
-                page_rounded[b] = big.tile([P, 4, T2], BF16, name="page_rounded", tag="big", align_bytes=64)
-            nc.scalar.copy(page_rounded[b][:, t, :], page[n][:])
+                page_rounded[b] = keep.tile([P, 4, T2], BF16, name="page_rounded", tag=("shifted", "turns")[b],
+                                            align_bytes=64)
+            nc.scalar.copy(page_rounded[b][:, t, ms], page[n][:, ms])
 
         def magnitude(n):
-            nc.scalar.activation(amp_t[n][:], amp_t[n][:], ACT.Abs)
+            nc.scalar.activation(cols[n][:], cols[n][:], ACT.Abs)
+
+        def x_by_tensor(n):
+            b, t = divmod(n, 4)
+            turned = psum.tile([P, PX], F32, name="turned", tag="sum", bufs=2)
+            for c in range(4):
+                js = slice(P * c, P * (c + 1))
+                nc.tensor.matmul(turned[:, js], lhsT=cols[n][:, js], rhs=ident[:], is_transpose=True,
+                                 start=True, stop=False)
+                nc.tensor.matmul(turned[:, js], lhsT=base_t[b][:, t, js], rhs=ident[:], is_transpose=True,
+                                 start=False, stop=True)
+            nc.scalar.copy(cols[n][:], turned[:])
+            back = psum.tile([P, PX], F32, name="back", tag="sum", bufs=2)
+            for c in range(4):
+                js = slice(P * c, P * (c + 1))
+                nc.tensor.transpose(back[:, js], cols[n][:, js], ident[:])
+            nc.scalar.activation(x_rounded[b][:, t, :], back[:], ACT.Copy, scale=qv_c[:, b, t : t + 1])
+
+        def scale_base(n):
+            b, t = divmod(n, 4)
+            nc.scalar.activation(base_t[b][:, t, :], base_t[b][:, t, :], ACT.Copy, scale=qv_c[:, b, t : t + 1])
+
+        def x_by_vector(n):
+            b, t = divmod(n, 4)
+            nc.vector.scalar_tensor_tensor(x_rounded[b][:, t, :], cols[n][:], qv_c[:, b, t : t + 1], base_t[b][:, t, :],
+                                           ALU.mult, ALU.add)
+
+        def weave(copy, dst, src, piece):
+            cs = slice(WEAVE * piece, WEAVE * (piece + 1))
+            copy(dst[:, cs, :], src[:, :, cs].rearrange("p t c -> p c t"))
+
+        def quantise(codes, scales, woven):
+            nc.vector.quantize_mx(out=codes.bitcast(FP8X4), scales=scales, in_=woven.rearrange("p c t -> p (c t)"))
 
         page_c = {1: keep.tile([P, T2], U32, name="page_c1", align_bytes=64)}
         page_s = keep.tile([P, 2, T2], U8, name="page_s", align_bytes=64)
         x_c = {1: keep.tile([P, PX], U32, name="x_c1", align_bytes=64)}
         x_s = keep.tile([P, 2, PX], U8, name="x_s", align_bytes=64)
 
-        def weave_cols(dst, src, cols, on_vector):
-            s = src[:, :, cols].rearrange("p t c -> p c t")
-            if on_vector:
-                nc.vector.tensor_copy(dst[:, cols, :], s)
-            else:
-                nc.scalar.copy(dst[:, cols, :], s)
-
-        woven = {}
-
-        def weave_first_half(k):
-            if k == 0:
-                woven["p"] = big.tile([P, T2, 4], BF16, name="page_g", tag="big", align_bytes=64)
-            if k == 4:
-                woven["x"] = mid.tile([P, PX, 4], BF16, name="x_g", tag="mid", align_bytes=64)
-            if k < 4:
-                weave_cols(woven["p"], page_rounded[0], slice(256 * k, 256 * (k + 1)), False)
-            else:
-                weave_cols(woven["x"], x_rounded[0], slice(256 * (k - 4), 256 * (k - 3)), XW_V)
-
-        def quant_page_first():
-            page_c[0] = keep.tile([P, T2], U32, name="page_c0", tag="work%d" % HOLD_P, align_bytes=64)
-            nc.vector.quantize_mx(out=page_c[0][:].bitcast(FP8X4), scales=page_s[:, 0, :], in_=woven["p"][:].rearrange("p c t -> p (c t)"))
-
-        def quant_x_first():
-            x_c[0] = keep.tile([P, PX], U32, name="x_c0", tag="work%d" % HOLD_X, align_bytes=64)
-            nc.vector.quantize_mx(out=x_c[0][:].bitcast(FP8X4), scales=x_s[:, 0, :], in_=woven["x"][:].rearrange("p c t -> p (c t)"))
-
-        def scale_base(n):
-            b, t = divmod(n, 4)
-            nc.scalar.activation(base_t[b][:, t, :], base_t[b][:, t, :], ACT.Copy, scale=qv_c[:, b, t : t + 1])
-
-        def finish_x(n, js):
-            b, t = divmod(n, 4)
-            if t == 0:
-                x_rounded[b] = mid.tile([P, 4, PX], BF16, name="x_rounded", tag="mid", align_bytes=64)
-            nc.vector.scalar_tensor_tensor(x_rounded[b][:, t, js], amp_t[n][:, js], qv_c[:, b, t : t + 1], base_t[b][:, t, js], ALU.mult, ALU.add)
-
-        def last_tile():
-            b, t, n = 1, 3, 7
-            g = big.tile([P, T2, 4], BF16, name="page_g", tag="big", align_bytes=64)
-            gx = mid.tile([P, PX, 4], BF16, name="x_g", tag="mid", align_bytes=64)
-            halves = [slice(256 * half, 256 * (half + 1)) for half in range(2)]
-            col = amp_t[n]
-            for half, js in enumerate(halves):
-                nc.vector.tensor_copy(col[:, js], page[n][:].indirect(list3[:, 16 * half : 16 * (half + 1)]))
-            for js in halves:
-                nc.vector.scalar_tensor_tensor(col[:, js], col[:, js], -1.0, col[:, js], ALU.mult, ALU.max)
-            for js in halves:
-                finish_x(n, js)
-            for js in halves:
-                weave_cols(gx, x_rounded[b], js, True)
-            for half, js in enumerate(halves):
-                cols = slice(512 * half, 512 * (half + 1))
-                nc.scalar.copy(page_rounded[b][:, t, cols], page[n][:, cols])
-                for quarter in (2 * half, 2 * half + 1):
-                    weave_cols(g, page_rounded[b], slice(256 * quarter, 256 * (quarter + 1)), quarter >= 4 - VQ)
-                nc.vector.quantize_mx(out=x_c[b][:, js].bitcast(FP8X4), scales=x_s[:, b, js],
-                                      in_=gx[:, js, :].rearrange("p c t -> p (c t)"))
-            for half in range(2):
-                cols = slice(512 * half, 512 * (half + 1))
-                nc.vector.quantize_mx(out=page_c[b][:, cols].bitcast(FP8X4), scales=page_s[:, b, cols],
-                                      in_=g[:, cols, :].rearrange("p c t -> p (c t)"))
-
-        def after(n):
-            scale_base(n)
-            magnitude(n)
-            finish_x(n, slice(0, PX))
-            round_page(n)
-
-        weave_w1(0, 0, W0_V)
+        weave_w1(0, 0)
         angles(0)
-        read_angles(0, slice(0, 1), range(4), True)
-        sines(GROUPS[0])
-        weave_w1(0, 1, True)
-        quant_w1(0, 0)
-        quant_w1(0, 1)
-        read_angles(0, slice(1, 4), range(4), False)
-        for k, group in enumerate(GROUPS):
-            for step in (times_amp, direct, put, pick):
-                for n in group:
-                    if step is not pick or n < 7:
-                        step(n)
-            if k == ANG_AT:
-                angles(1)
-                read_angles(1, slice(0, 4), range(4), False)
-            if k == W1_AT:
-                weave_w1(1, 0, False)
-                quant_w1(1, 0)
-                weave_w1(1, 1, False)
-                quant_w1(1, 1)
-            if k + 1 < len(GROUPS):
-                sines(GROUPS[k + 1])
-            if k >= LAG:
-                for n in GROUPS[k - LAG]:
-                    after(n)
-                if 3 in GROUPS[k - LAG]:
-                    for piece in range(6):
-                        weave_first_half(piece)
-        for group in GROUPS[len(GROUPS) - LAG :]:
-            for n in group:
-                if n < 7:
-                    after(n)
-        scale_base(7)
-        quant_page_first()
-        quant_x_first()
-        last_tile()
+        read_angles(0, slice(0, 1), True)
+        sines(0)
+        weave_w1(0, 1)
+        quantise_w1(0, 0)
+        quantise_w1(0, 1)
+        read_angles(0, slice(1, 4), False)
+        sines(1)
+        sines(2, 3)
+        angles(1)
+        read_angles(1, slice(0, 4), False)
+        sines(4, 5)
+        sines(6, 7)
+        change_page(0)
+        for a in range(2):
+            weave_w1(1, a)
+            quantise_w1(1, a)
+        change_page(1)
+        change_page(2, 3)
+        for n in range(4):
+            magnitude(n)
+            round_page(n)
+        for n in range(4, TILES):
+            scale_base(n)
+        change_page(4, 5)
+        page_woven = big.tile([P, T2, 4], BF16, name="page_woven", tag="big", align_bytes=64)
+        x_rounded[0] = mid.tile([P, 4, PX], BF16, name="x_rounded", tag="mid", align_bytes=64)
+        for n in range(4):
+            x_by_tensor(n)
+            weave(nc.scalar.copy, page_woven, page_rounded[0], n)
+        change_page(6, 7)
+        x_woven = mid.tile([P, PX, 4], BF16, name="x_woven", tag="mid", align_bytes=64)
+        x_rounded[1] = mid.tile([P, 4, PX], BF16, name="x_rounded", tag="mid", align_bytes=64)
+        for n in range(4, TILES - 1):
+            magnitude(n)
+            x_by_vector(n)
+            if n - 4 < PX // WEAVE:
+                weave(nc.scalar.copy, x_woven, x_rounded[0], n - 4)
+            round_page(n)
+        page_c[0] = keep.tile([P, T2], U32, name="page_c0", tag="work5", align_bytes=64)
+        quantise(page_c[0][:], page_s[:, 0, :], page_woven[:])
+        x_c[0] = keep.tile([P, PX], U32, name="x_c0", tag="work6", align_bytes=64)
+        quantise(x_c[0][:], x_s[:, 0, :], x_woven[:])
 
-        for c in range(8):
-            tag, bufs = (("angle", 4), ("angle", 4), ("rest", 2), ("acc_a", 2))[c // 2]
-            acc = psum.tile([P, PX], F32, name="acc_o", tag=tag, bufs=bufs)
-            cols = slice(P * c, P * (c + 1))
+        last = TILES - 1
+        page_woven = big.tile([P, T2, 4], BF16, name="page_woven", tag="big", align_bytes=64)
+        x_woven = mid.tile([P, PX, 4], BF16, name="x_woven", tag="mid", align_bytes=64)
+        magnitude(last)
+        x_by_vector(last)
+        for piece in range(2):
+            weave(nc.vector.tensor_copy, x_woven, x_rounded[1], piece)
+        for half in range(2):
+            round_page(last, slice(2 * WEAVE * half, 2 * WEAVE * (half + 1)))
+            for piece in (2 * half, 2 * half + 1):
+                weave(nc.vector.tensor_copy if piece == 3 else nc.scalar.copy, page_woven, page_rounded[1], piece)
+            js = slice(WEAVE * half, WEAVE * (half + 1))
+            quantise(x_c[1][:, js], x_s[:, 1, js], x_woven[:, js, :])
+        for half in range(2):
+            ms = slice(2 * WEAVE * half, 2 * WEAVE * (half + 1))
+            quantise(page_c[1][:, ms], page_s[:, 1, ms], page_woven[:, ms, :])
+
+        banks = [("angle", 4)] * 4 + [("rest", 2)] * 2 + [("sum", 2)] * 2
+        for c, (tag, bufs) in enumerate(banks):
+            acc = psum.tile([P, PX], F32, name="score", tag=tag, bufs=bufs)
+            ms = slice(P * c, P * (c + 1))
             for b in range(2):
-                nc.tensor.matmul_mx(acc[:], lhsT=page_c[b][:, cols].bitcast(FP8X4), lhsT_scale=page_s[:, b, cols],
-                                    rhs=x_c[b][:].bitcast(FP8X4), rhs_scale=x_s[:, b, :], start=(b == 0), stop=(b == 1))
-            res = amp_t[c]
-            nc.vector.tensor_scalar(res[:], acc[:], slot_c[:, c : c + 1], None, ALU.max)
-            nc.sync.dma_start(out[cols, :], res[:])
+                nc.tensor.matmul_mx(acc[:], lhsT=page_c[b][:, ms].bitcast(FP8X4), lhsT_scale=page_s[:, b, ms],
+                                    rhs=x_c[b][:].bitcast(FP8X4), rhs_scale=x_s[:, b, :],
+                                    start=(b == 0), stop=(b == 1))
+            nc.vector.tensor_scalar(cols[c][:], acc[:], slot_c[:, c : c + 1], None, ALU.max)
+            nc.sync.dma_start(out[ms, :], cols[c][:])

import math
from contextlib import ExitStack

import concourse.mybir as mybir
from concourse.masks import make_identity

K, T, S, H, T2, PX = 1024, 2048, 512, 1024, 1024, 512
FLOPS = 2 * K * H * S * 2 + 2 * H * T2 * PX

F32 = mybir.dt.float32
BF16 = mybir.dt.bfloat16
I32 = mybir.dt.int32
U32 = mybir.dt.uint32
U16 = mybir.dt.uint16
U8 = mybir.dt.uint8
FP8X4 = mybir.dt.float8_e4m3fn_x4
FP4X4 = mybir.dt.float4_e2m1fn_x4
ALU = mybir.AluOpType
ACT = mybir.ActivationFunctionType

P = 128
PASS = 512
TILES = 8
TWO_PI = 2.0 * math.pi
ROUNDER = 1.5 * 2.0**23
WEAVE = 256


def tile_list_blade_noise_page_kernel(tc, tab_words, tab_scales, offs, w1, w4_words, w4_scales, amp, gain,
                                                page0, wgs, offs2, offs3, base, qv, slot, out):
    nc = tc.nc
    with ExitStack() as ctx:
        keep = ctx.enter_context(tc.tile_pool(name="keep", bufs=1))
        big = ctx.enter_context(tc.tile_pool(name="big", bufs=6))
        mid = ctx.enter_context(tc.tile_pool(name="mid", bufs=4))
        psum = ctx.enter_context(tc.psum_pool(name="psum", bufs=1))

        warm = keep.tile([P, 1], F32, name="warm")
        nc.vector.memset(warm[:], 0.0)
        nc.scalar.activation(warm[:], warm[:], ACT.Sin)

        tab_s = keep.tile([P, 2, T], U8, name="tab_s", align_bytes=64)
        w4_s = keep.tile([P, 2, H], U8, name="w4_s", align_bytes=64)
        nc.vector.memset(tab_s[:].rearrange("p a n -> p (a n)").bitcast(I32), 0)
        nc.gpsimd.memset(w4_s[:].rearrange("p a n -> p (a n)").bitcast(I32), 0)
        ident = keep.tile([P, P], F32, name="ident")
        make_identity(nc, ident[:])

        list1 = keep.tile([P, S // 16], U16, name="list1")
        list2 = keep.tile([P, S // 16], U16, name="list2")
        list3 = keep.tile([P, PX // 16], U16, name="list3")
        gain_c = keep.tile([P, 2, 4], F32, name="gain_c")
        qv_c = keep.tile([P, 2, 4], F32, name="qv_c")
        slot_c = keep.tile([P, T2 // P], F32, name="slot_c")
        wgs_first = keep.tile([P, S], F32, name="wgs_first")
        wgs_rest = keep.tile([P, 3, S], F32, name="wgs_rest")
        wgs_rows = wgs.rearrange("(p t) j -> p t j", t=4)
        tab_w = [big.tile([P, T], I32, name="tab_w", tag="big", align_bytes=64) for a in range(2)]
        w4_w = [keep.tile([P, 2, H], U8, name="w4_w%d" % b, align_bytes=64) for b in range(2)]
        w1_raw = {}

        def load_w4(b):
            half = w4_words[:, :, H * b : H * (b + 1)]
            nc.sync.dma_start(w4_w[b][:].bitcast(I32), half.rearrange("a p n -> p a n").bitcast(I32))

        def load_w1(b, a):
            w1_raw[b, a] = big.tile([P, 4, PASS], F32, name="w1_raw", tag="big", align_bytes=64)
            quarter = w1[PASS * a : PASS * (a + 1), PASS * b : PASS * (b + 1)]
            nc.sync.dma_start(w1_raw[b, a][:], quarter.rearrange("(p i) c -> p i c", i=4))

        def load_tab(a):
            nc.sync.dma_start(tab_w[a][:], tab_words[a].rearrange("p n i -> p (n i)").bitcast(I32))

        def load_scales(tile, rows):
            by_u = rows.rearrange("a (q u) n -> u q a n", u=4)
            for u in range(4):
                nc.sync.dma_start(tile[u:P:32, :, :].bitcast(I32), by_u[u].bitcast(I32))

        def load_wgs(tile, rows, quarters):
            for q in quarters:
                nc.sync.dma_start(tile[32 * q : 32 * (q + 1)], rows)

        nc.sync.dma_start(list1[:], offs)
        nc.sync.dma_start(list2[:], offs2)
        nc.sync.dma_start(list3[:], offs3)
        nc.sync.dma_start(gain_c[:], gain.rearrange("(b p t) -> p b t", b=2, t=4))
        nc.sync.dma_start(qv_c[:], qv.rearrange("(b p t) -> p b t", b=2, t=4))
        load_tab(0)
        load_wgs(wgs_first, wgs_rows[:, 0, :], (0, 1))
        load_scales(tab_s, tab_scales)
        load_tab(1)
        load_w4(0)
        load_scales(w4_s, w4_scales)
        load_w1(0, 0)
        load_w1(0, 1)

        amp_rows = amp.rearrange("(b p t) j -> b t p j", b=2, t=4)
        page_rows = page0.rearrange("(b p t) m -> b t p m", b=2, t=4)
        cols = [keep.tile([P, S], F32, name="cols%d" % n) for n in range(TILES)]
        page = [keep.tile([P, T2], F32, name="page%d" % n) for n in range(TILES)]
        base_t = [keep.tile([P, 4, PX], F32, name="base%d" % b) for b in range(2)]

        def load_amp(*tiles):
            for n in tiles:
                nc.sync.dma_start(cols[n][:], amp_rows[n // 4, n % 4])

        def load_page(*tiles):
            for n in tiles:
                nc.sync.dma_start(page[n][:], page_rows[n // 4, n % 4])

        def load_base(b):
            nc.sync.dma_start(base_t[b][:], base[PASS * b : PASS * (b + 1), :].rearrange("(p t) j -> p t j", t=4))

        load_amp(0)
        load_wgs(wgs_first, wgs_rows[:, 0, :], (2, 3))
        load_page(0)
        load_amp(1)
        load_wgs(wgs_rest, wgs_rows[:, 1:4, :], range(4))
        load_page(1)
        load_w4(1)
        load_amp(2, 3)
        load_page(2, 3)
        load_w1(1, 0)
        load_w1(1, 1)
        load_base(1)
        load_base(0)
        load_page(4, 5)
        load_amp(4, 5)
        load_page(6, 7)
        load_amp(6, 7)
        with nc.allow_non_contiguous_dma(reason="one value a partition"):
            nc.sync.dma_start(slot_c[:], slot.rearrange("(c p) -> p c", p=P))

        v_w = keep.tile([P, 2, S], U32, name="v_w", align_bytes=64)
        v_s = keep.tile([P, 2, S], U8, name="v_s", align_bytes=64)
        nc.vector.tensor_copy(v_w[:, 0, :], tab_w[0][:].bitcast(U32).indirect(list1[:]))
        for a in range(2):
            nc.vector.tensor_copy(v_s[:, a, :], tab_s[:, a, :].indirect(list1[:]))
        nc.vector.tensor_copy(v_w[:, 1, :], tab_w[1][:].bitcast(U32).indirect(list1[:]))

        w1_c = keep.tile([P, 2, 2, PASS], U32, name="w1_c", align_bytes=64)
        w1_s = keep.tile([P, 2, 2, PASS], U8, name="w1_s", align_bytes=64)
        w1_woven = {}

        def weave_w1(b, a):
            w1_woven[b, a] = mid.tile([P, 4, P, 4], BF16, name="w1_woven", tag="mid", align_bytes=64)
            dst = w1_woven[b, a][:].rearrange("p t q i -> p q t i")
            src = w1_raw[b, a][:].rearrange("p i (q t) -> p q t i", t=4)
            if b == 0:
                nc.vector.tensor_copy(dst, src)
            else:
                for q0 in (0, P // 2):
                    nc.scalar.copy(dst[:, q0 : q0 + P // 2], src[:, q0 : q0 + P // 2])

        def quantise_w1(b, a):
            nc.vector.quantize_mx(out=w1_c[:, b, a, :].bitcast(FP8X4), scales=w1_s[:, b, a, :],
                                  in_=w1_woven[b, a][:].rearrange("p t q i -> p (t q i)"))

        work = [keep.tile([P, S], F32, name="work%d" % n, tag="work%d" % n, align_bytes=64) for n in range(TILES)]
        angle = {}
        turns = {}
        shifted = {}
        minus_whole = {}

        def angles(b):
            turns[b] = keep.tile([P, 4, 4, P], F32, name="turns", tag="turns", align_bytes=64)
            shifted[b] = keep.tile([P, 4, 4, P], U32, name="shifted", tag="shifted", align_bytes=64)
            minus_whole[b] = keep.tile([P, 4, 4, P], F32, name="minus_whole", tag="minus_whole")
            for c in range(4):
                angle[b, c] = psum.tile([P, PASS], F32, name="angle", tag="angle", bufs=4)
                js = slice(P * c, P * (c + 1))
                for a in range(2):
                    nc.tensor.matmul_mx(angle[b, c][:], lhsT=v_w[:, a, js].bitcast(FP8X4), lhsT_scale=v_s[:, a, js],
                                        rhs=w4_w[b][:, a, :].bitcast(FP4X4),
                                        rhs_scale=w4_s[:, a, PASS * b : PASS * (b + 1)],
                                        start=(a == 0), stop=(a == 1))

        def read_angles(b, ts, turns_on_vector):
            for c in range(4):
                src = angle[b, c][:].rearrange("j (q t) -> j t q", t=4)[:, ts, :]
                nc.scalar.activation(shifted[b][:, ts, c, :], src, ACT.Copy, bias=ROUNDER, scale=1.0 / TWO_PI)
                if turns_on_vector:
                    nc.vector.tensor_scalar(turns[b][:, ts, c, :], src, 1.0 / TWO_PI, None, ALU.mult)
                else:
                    nc.scalar.activation(turns[b][:, ts, c, :], src, ACT.Copy, scale=1.0 / TWO_PI)

        def sines(*tiles):
            rest = {}
            for n in tiles:
                b, t = divmod(n, 4)
                if b == 0:
                    nc.vector.tensor_scalar(minus_whole[b][:, t], shifted[b][:, t].bitcast(I32), -1.0, ROUNDER,
                                            ALU.mult, ALU.add)
                else:
                    nc.scalar.activation(minus_whole[b][:, t], shifted[b][:, t], ACT.Copy, bias=ROUNDER, scale=-1.0)
                rest[n] = psum.tile([P, S], F32, name="rest", tag="rest", bufs=2)
            for c in range(4):
                js = slice(P * c, P * (c + 1))
                for n in tiles:
                    b, t = divmod(n, 4)
                    nc.tensor.matmul(rest[n][:, js], lhsT=turns[b][:, t, c, :], rhs=ident[:], is_transpose=True,
                                     start=True, stop=False)
                    nc.tensor.matmul(rest[n][:, js], lhsT=minus_whole[b][:, t, c, :], rhs=ident[:], is_transpose=True,
                                     start=False, stop=True)
            for n in tiles:
                nc.scalar.activation(work[n][:], rest[n][:], ACT.Sin, scale=TWO_PI)

        def times_amp(n):
            b, t = divmod(n, 4)
            nc.vector.scalar_tensor_tensor(work[n][:], work[n][:], gain_c[:, b, t : t + 1], cols[n][:],
                                           ALU.mult, ALU.mult)

        def plus_direct(n):
            b, t = divmod(n, 4)
            acc = psum.tile([P, S], F32, name="direct", tag="angle" if b else "sum", bufs=4 if b else 2)
            rs = slice(P * t, P * (t + 1))
            for a in range(2):
                nc.tensor.matmul_mx(acc[:], lhsT=w1_c[:, b, a, rs].bitcast(FP8X4), lhsT_scale=w1_s[:, b, a, rs],
                                    rhs=v_w[:, a, :].bitcast(FP8X4), rhs_scale=v_s[:, a, :],
                                    start=(a == 0), stop=(a == 1))
            nc.vector.scalar_tensor_tensor(work[n][:], acc[:], gain_c[:, b, t : t + 1], work[n][:], ALU.mult, ALU.add)

        def put(n):
            t = n % 4
            factor = wgs_first[:] if t == 0 else wgs_rest[:, t - 1, :]
            nc.vector.tensor_tensor(page[n][:].indirect(list2[:]), work[n][:], factor, ALU.mult)

        def pick(n):
            nc.vector.tensor_copy(cols[n][:], page[n][:].indirect(list3[:]))

        def change_page(*tiles):
            for step in (times_amp, plus_direct, put, pick):
                for n in tiles:
                    step(n)

        page_rounded = {}
        x_rounded = {}

        def round_page(n, ms=slice(0, T2)):
            b, t = divmod(n, 4)
            if t == 0:
                page_rounded[b] = keep.tile([P, 4, T2], BF16, name="page_rounded", tag=("shifted", "turns")[b],
                                            align_bytes=64)
            nc.scalar.copy(page_rounded[b][:, t, ms], page[n][:, ms])

        def magnitude(n):
            nc.scalar.activation(cols[n][:], cols[n][:], ACT.Abs)

        def x_by_tensor(n):
            b, t = divmod(n, 4)
            turned = psum.tile([P, PX], F32, name="turned", tag="sum", bufs=2)
            for c in range(4):
                js = slice(P * c, P * (c + 1))
                nc.tensor.matmul(turned[:, js], lhsT=cols[n][:, js], rhs=ident[:], is_transpose=True,
                                 start=True, stop=False)
                nc.tensor.matmul(turned[:, js], lhsT=base_t[b][:, t, js], rhs=ident[:], is_transpose=True,
                                 start=False, stop=True)
            nc.scalar.copy(cols[n][:], turned[:])
            back = psum.tile([P, PX], F32, name="back", tag="sum", bufs=2)
            for c in range(4):
                js = slice(P * c, P * (c + 1))
                nc.tensor.transpose(back[:, js], cols[n][:, js], ident[:])
            nc.scalar.activation(x_rounded[b][:, t, :], back[:], ACT.Copy, scale=qv_c[:, b, t : t + 1])

        def scale_base(n):
            b, t = divmod(n, 4)
            nc.scalar.activation(base_t[b][:, t, :], base_t[b][:, t, :], ACT.Copy, scale=qv_c[:, b, t : t + 1])

        def x_by_vector(n):
            b, t = divmod(n, 4)
            nc.vector.scalar_tensor_tensor(x_rounded[b][:, t, :], cols[n][:], qv_c[:, b, t : t + 1], base_t[b][:, t, :],
                                           ALU.mult, ALU.add)

        def weave(copy, dst, src, piece):
            cs = slice(WEAVE * piece, WEAVE * (piece + 1))
            copy(dst[:, cs, :], src[:, :, cs].rearrange("p t c -> p c t"))

        def quantise(codes, scales, woven):
            nc.vector.quantize_mx(out=codes.bitcast(FP8X4), scales=scales, in_=woven.rearrange("p c t -> p (c t)"))

        page_c = {1: keep.tile([P, T2], U32, name="page_c1", align_bytes=64)}
        page_s = keep.tile([P, 2, T2], U8, name="page_s", align_bytes=64)
        x_c = {1: keep.tile([P, PX], U32, name="x_c1", align_bytes=64)}
        x_s = keep.tile([P, 2, PX], U8, name="x_s", align_bytes=64)

        weave_w1(0, 0)
        angles(0)
        read_angles(0, slice(0, 1), True)
        sines(0)
        weave_w1(0, 1)
        quantise_w1(0, 0)
        quantise_w1(0, 1)
        read_angles(0, slice(1, 4), False)
        sines(1)
        sines(2, 3)
        angles(1)
        read_angles(1, slice(0, 4), False)
        sines(4, 5)
        sines(6, 7)
        change_page(0)
        for a in range(2):
            weave_w1(1, a)
            quantise_w1(1, a)
        change_page(1)
        change_page(2, 3)
        for n in range(4):
            magnitude(n)
            round_page(n)
        for n in range(4, TILES):
            scale_base(n)
        change_page(4, 5)
        page_woven = big.tile([P, T2, 4], BF16, name="page_woven", tag="big", align_bytes=64)
        x_rounded[0] = mid.tile([P, 4, PX], BF16, name="x_rounded", tag="mid", align_bytes=64)
        for n in range(4):
            x_by_tensor(n)
            weave(nc.scalar.copy, page_woven, page_rounded[0], n)
        change_page(6, 7)
        x_woven = mid.tile([P, PX, 4], BF16, name="x_woven", tag="mid", align_bytes=64)
        x_rounded[1] = mid.tile([P, 4, PX], BF16, name="x_rounded", tag="mid", align_bytes=64)
        for n in range(4, TILES - 1):
            magnitude(n)
            x_by_vector(n)
            if n - 4 < PX // WEAVE:
                weave(nc.scalar.copy, x_woven, x_rounded[0], n - 4)
            round_page(n)
        page_c[0] = keep.tile([P, T2], U32, name="page_c0", tag="work5", align_bytes=64)
        quantise(page_c[0][:], page_s[:, 0, :], page_woven[:])
        x_c[0] = keep.tile([P, PX], U32, name="x_c0", tag="work6", align_bytes=64)
        quantise(x_c[0][:], x_s[:, 0, :], x_woven[:])

        last = TILES - 1
        page_woven = big.tile([P, T2, 4], BF16, name="page_woven", tag="big", align_bytes=64)
        x_woven = mid.tile([P, PX, 4], BF16, name="x_woven", tag="mid", align_bytes=64)
        magnitude(last)
        x_by_vector(last)
        for piece in range(2):
            weave(nc.vector.tensor_copy, x_woven, x_rounded[1], piece)
        for half in range(2):
            round_page(last, slice(2 * WEAVE * half, 2 * WEAVE * (half + 1)))
            for piece in (2 * half, 2 * half + 1):
                weave(nc.vector.tensor_copy if piece == 3 else nc.scalar.copy, page_woven, page_rounded[1], piece)
            js = slice(WEAVE * half, WEAVE * (half + 1))
            quantise(x_c[1][:, js], x_s[:, 1, js], x_woven[:, js, :])
        for half in range(2):
            ms = slice(2 * WEAVE * half, 2 * WEAVE * (half + 1))
            quantise(page_c[1][:, ms], page_s[:, 1, ms], page_woven[:, ms, :])

        banks = [("angle", 4)] * 4 + [("rest", 2)] * 2 + [("sum", 2)] * 2
        for c, (tag, bufs) in enumerate(banks):
            acc = psum.tile([P, PX], F32, name="score", tag=tag, bufs=bufs)
            ms = slice(P * c, P * (c + 1))
            for b in range(2):
                nc.tensor.matmul_mx(acc[:], lhsT=page_c[b][:, ms].bitcast(FP8X4), lhsT_scale=page_s[:, b, ms],
                                    rhs=x_c[b][:].bitcast(FP8X4), rhs_scale=x_s[:, b, :],
                                    start=(b == 0), stop=(b == 1))
            nc.vector.tensor_scalar(cols[c][:], acc[:], slot_c[:, c : c + 1], None, ALU.max)
            nc.sync.dma_start(out[ms, :], cols[c][:])
